import numpy as np
import ml_dtypes


def mxq(x, axis, fmt="e4m3"):
    dtype, down = {"e4m3": (ml_dtypes.float8_e4m3fn, 7), "e5m2": (ml_dtypes.float8_e5m2, 14)}[fmt]
    v = np.moveaxis(np.asarray(x, np.float32).astype(ml_dtypes.bfloat16).astype(np.float64), axis, -1)
    blocks = v.reshape(v.shape[:-1] + (-1, 32))
    amax = np.abs(blocks).max(-1, keepdims=True)
    byte = np.maximum(np.where(amax > 0, np.frexp(amax)[1] - 1 + 127, 0) - down, 1)
    scale = np.exp2(byte - 127.0)
    codes = (blocks / scale).astype(np.float32).astype(dtype).astype(np.float64)
    return np.moveaxis((codes * scale).reshape(v.shape), -1, axis)


WIDE = False


def mx_kscale(k):
    if not WIDE:
        return np.ones(k)
    levels = np.array([10, -10, 5, -5, 0])
    if k % 512:
        return np.exp2(np.random.permutation(np.resize(levels, k // 32))).repeat(32)
    a = np.empty((k // 512, 16))
    for p in range(k // 512):
        a[p, :8] = np.random.permutation(np.resize(levels, 8))
        for g in range(8):
            far = levels[np.abs(levels - a[p, g]) >= 10]
            a[p, g + 8] = far[np.random.randint(len(far))]
    return np.exp2(a.ravel()).repeat(32)


def f64(x):
    return np.asarray(x).astype(np.float64)


def striped(idx):
    return np.tile(idx.reshape(-1, 16).T, (8, 1)).astype(np.uint16)


def unstriped(offs):
    return offs[:16].T.reshape(-1).astype(np.int64)


def pack_weight(w):
    k, n = w.shape
    w = f64(np.asarray(w, np.float32).astype(ml_dtypes.bfloat16)).reshape(k // 32, 32, n)
    amax = np.abs(w).max(1)
    byte = np.clip(np.where(amax > 0, np.frexp(amax)[1] - 1 + 127 - 7, 1), 1, 254)
    scaled = (w * np.exp2(127.0 - byte)[:, None, :]).reshape(k, n).astype(np.float32)
    words = np.ascontiguousarray(scaled.reshape(k // 512, 128, 4, n).transpose(0, 1, 3, 2)).astype(ml_dtypes.float8_e4m3fn).view(np.uint8)
    return words, np.ascontiguousarray(byte.astype(np.uint8).reshape(k // 512, 16, n))


def unpack_weight(words, scales):
    g, p, n, _ = words.shape
    vals = np.ascontiguousarray(words).view(ml_dtypes.float8_e4m3fn).astype(np.float64) * np.repeat(np.exp2(scales.astype(np.float64) - 127.0), 8, axis=1)[..., None]
    return vals.transpose(0, 1, 3, 2).reshape(g * 512, n)


def relu(v):
    return np.maximum(v, 0.0)


K, T, S, V, H, N = 1024, 2048, 1024, 512, 512, 256


def setup_inputs():
    n = np.random.standard_normal
    s = mx_kscale(K)[:, None]
    u = mx_kscale(H)
    packed_w2 = pack_weight(n((H, N)) / np.sqrt(2 * H) / u[:, None])
    packed_w3 = pack_weight(n((H, N)) / np.sqrt(2 * H) / u[:, None])
    return {
        "xT": (n((K, T)) * s).astype(np.float32),
        "w1": (n((K, H)) / np.sqrt(K) / s * u).astype(np.float32),
        "w2_words": packed_w2[0],
        "w2_scales": packed_w2[1],
        "w3_words": packed_w3[0],
        "w3_scales": packed_w3[1],
        "offs": striped(np.random.permutation(T)[:S]),
        "cen": striped(np.random.permutation(S)[:V]),
        "pos1": striped(np.random.permutation(S)[:V]),
        "pos2": striped(np.random.permutation(S)[:V]),
        "pos3": striped(np.random.permutation(S)[:V]),
        "pos4": striped(np.random.permutation(S)[:V]),
    }


def reference(xT, w1, w2_words, w2_scales, w3_words, w3_scales, offs, cen, pos1, pos2, pos3, pos4):
    xq = mxq(f64(xT)[:, unstriped(offs)], 0, "e4m3")
    h = relu(mxq(f64(w1), 0, "e4m3").T @ xq)
    hc = h[:, unstriped(cen)]
    z = (h[:, unstriped(pos1)] + h[:, unstriped(pos2)] + h[:, unstriped(pos3)] + h[:, unstriped(pos4)]) / 4
    return unpack_weight(w2_words, w2_scales).T @ mxq(hc, 0, "e4m3") + unpack_weight(w3_words, w3_scales).T @ mxq(z, 0, "e4m3")

@@ -1,0 +1,278 @@
+from contextlib import ExitStack
+
+import concourse.mybir as mybir
+from concourse.masks import make_identity
+
+K, T, S, V, H, N = 1024, 2048, 1024, 512, 512, 256
+FLOPS = 2 * K * H * S + 2 * 2 * H * N * V
+
+F32 = mybir.dt.float32
+BF16 = mybir.dt.bfloat16
+I32 = mybir.dt.int32
+U32 = mybir.dt.uint32
+U16 = mybir.dt.uint16
+U8 = mybir.dt.uint8
+FP8X4 = mybir.dt.float8_e4m3fn_x4
+COPY = mybir.ActivationFunctionType.Copy
+RELU = mybir.ActivationFunctionType.Relu
+
+P = 128
+PACK = 4
+K_PASS = P * PACK
+BANK = 512
+X_CHUNKS = ((1024, 1024), (512, 512, 512, 256, 256))
+UNIT = 512
+VECTOR_SHARE = 3
+PIECES = ((0, 256), (256, 384), (384, 512))
+
+
+def tile_picked_sagecat_mean_e_kernel(
+    tc, xT, w1, w2_words, w2_scales, w3_words, w3_scales, offs, cen, pos1, pos2, pos3, pos4, out
+):
+    nc = tc.nc
+    passes = K // K_PASS
+    with ExitStack() as ctx:
+        keep = ctx.enter_context(tc.tile_pool(name="keep", bufs=1))
+        ring = ctx.enter_context(tc.tile_pool(name="ring", bufs=4))
+        picked = ctx.enter_context(tc.tile_pool(name="picked", bufs=1))
+        psum = ctx.enter_context(tc.psum_pool(name="psum", bufs=1))
+
+        def bank(b, shape, name):
+            return psum.tile(shape, F32, name=name, tag=f"bank{b}")
+
+        def load_list(src, name):
+            t = keep.tile(list(src.shape), U16, name=name)
+            nc.sync.dma_start(t[:], src)
+            return t
+
+        x_bytes = keep.tile([P, T], U8, align_bytes=64)
+        nc.vector.memset(x_bytes[:].bitcast(I32), 0)
+        w23_scales = keep.tile([P, 2 * N], U8, align_bytes=64)
+        nc.vector.memset(w23_scales[:].bitcast(I32), 0)
+        ident = keep.tile([P, P], F32)
+        make_identity(nc, ident[:])
+
+        x_raw = {}
+        offs_t = None
+        for g in range(passes):
+            rows = xT[g * K_PASS : (g + 1) * K_PASS, :].rearrange("(p j) c -> p j c", j=PACK)
+            c0 = 0
+            for n in X_CHUNKS[g]:
+                raw = keep.tile([P, PACK, n], F32, name=f"x_raw_{g}_{c0}")
+                nc.sync.dma_start(raw[:], rows[:, :, c0 : c0 + n])
+                x_raw[g, c0] = raw
+                c0 = c0 + n
+            if g == 0:
+                offs_t = load_list(offs, "offs_t")
+        w_raw = []
+        for g in range(passes):
+            raw = keep.tile([P, PACK, H], F32, name=f"w_raw_{g}")
+            nc.sync.dma_start(raw[:], w1[g * K_PASS : (g + 1) * K_PASS, :].rearrange("(p j) c -> p j c", j=PACK))
+            w_raw.append(raw)
+        pos_t = [load_list(src, f"pos_t{d}") for d, src in enumerate((pos1, pos2, pos3, pos4))]
+        cen_t = load_list(cen, "cen_t")
+        w23_words = []
+        for a, (words, scales) in enumerate(((w2_words, w2_scales), (w3_words, w3_scales))):
+            wt = keep.tile([P, N], I32, name=f"w23_words{a}", align_bytes=64)
+            nc.sync.dma_start(wt[:], words[0].rearrange("p n t -> p (n t)").bitcast(I32))
+            w23_words.append(wt)
+        for a, (words, scales) in enumerate(((w2_words, w2_scales), (w3_words, w3_scales))):
+            for q in range(4):
+                nc.sync.dma_start(
+                    w23_scales[32 * q : 32 * q + 4, a * N : (a + 1) * N].bitcast(I32),
+                    scales[0, 4 * q : 4 * q + 4, :].bitcast(I32),
+                )
+
+        x_words = [keep.tile([P, T], U32, name=f"x_words{g}", align_bytes=64) for g in range(passes)]
+        g_words = {}
+
+        def gather_words(g, half, tag=None):
+            t = picked.tile([P, BANK], U32, name=f"g_words{g}_{half}", tag=tag or f"g_words{g}_{half}", align_bytes=64)
+            nc.vector.tensor_copy(t[:], x_words[g][:].indirect(offs_t[:, half * 32 : (half + 1) * 32]))
+            g_words[g, half] = t
+
+        for g in range(passes):
+            c0 = 0
+            for n in X_CHUNKS[g]:
+                raw = x_raw[g, c0]
+                m = min(n, UNIT)
+                for u0 in range(0, n, m):
+                    gt = ring.tile([P, m, PACK], BF16, name="x_grouped", align_bytes=64)
+                    cut = m * (5 if g == passes - 1 and c0 + n == T else VECTOR_SHARE) // 8
+                    nc.vector.tensor_copy(gt[:, :cut], raw[:, :, u0 : u0 + cut].rearrange("p j c -> p c j"))
+                    nc.scalar.activation(
+                        gt[:, cut:].rearrange("p (c i) j -> p c j i", i=4),
+                        raw[:, :, u0 + cut : u0 + m].rearrange("p j (c i) -> p c j i", i=4),
+                        COPY,
+                    )
+                    cols = slice(c0 + u0, c0 + u0 + m)
+                    nc.vector.quantize_mx(
+                        out=x_words[g][:, cols].bitcast(FP8X4),
+                        scales=x_bytes[4 * g : P, cols],
+                        in_=gt[:].rearrange("p c j -> p (c j)"),
+                    )
+                c0 = c0 + n
+            if g == 0:
+                gather_words(0, 0)
+                gather_words(0, 1)
+        g_bytes = keep.tile([P, S], U8, align_bytes=64)
+        nc.vector.tensor_copy(g_bytes[:], x_bytes[:].indirect(offs_t[:]))
+        gather_words(1, 0)
+
+        w_grouped, w_words, w_bytes = {}, {}, {}
+
+        def cast_w(g, t0, t1):
+            src = w_raw[g][:].rearrange("p j (m t) -> p m t j", t=PACK)
+            gt = picked.tile([P, t1 - t0, P, PACK], BF16, name=f"w_grouped{g}_{t0}", tag=f"w_grouped{g}_{t0}", align_bytes=64)
+            nc.scalar.activation(gt[:].rearrange("p t m j -> p m t j"), src[:, :, t0:t1, :], COPY)
+            w_grouped[g, t0] = gt
+
+        def quant_w(g, t0, t1, tag=None):
+            n = (t1 - t0) * P
+            words = keep.tile([P, n], U32, name=f"w_words{g}_{t0}", align_bytes=64)
+            scales = picked.tile([P, n], U8, name=f"w_bytes{g}_{t0}", tag=tag or f"w_bytes{g}_{t0}", align_bytes=64)
+            nc.vector.quantize_mx(
+                out=words[:].bitcast(FP8X4),
+                scales=scales[:],
+                in_=w_grouped[g, t0][:].rearrange("p t m j -> p (t m j)"),
+            )
+            for t in range(t0, t1):
+                w_words[g, t] = words[:, (t - t0) * P : (t - t0 + 1) * P]
+                w_bytes[g, t] = scales[:, (t - t0) * P : (t - t0 + 1) * P]
+
+        h = {}
+
+        def make_h(t):
+            ht = keep.tile([P, S], F32, name=f"h{t}")
+            acc = [bank(2 * (t // 2) + half, [P, BANK], f"h_acc{t}_{half}") for half in range(2)]
+            for g in range(passes):
+                for half in range(2):
+                    nc.tensor.matmul_mx(
+                        out=acc[half][:],
+                        lhsT=w_words[g, t].bitcast(FP8X4),
+                        lhsT_scale=w_bytes[g, t],
+                        rhs=g_words[g, half][:].bitcast(FP8X4),
+                        rhs_scale=g_bytes[4 * g : P, half * BANK : (half + 1) * BANK],
+                        start=(g == 0),
+                        stop=(g == passes - 1),
+                    )
+            for half in range(2):
+                dst = ht[:, half * BANK : (half + 1) * BANK]
+                if t == 0 and half == 1:
+                    nc.vector.tensor_scalar_max(dst, acc[half][:], 0.0)
+                else:
+                    nc.scalar.activation(dst, acc[half][:], RELU)
+            h[t] = ht
+
+        cast_w(0, 0, 1)
+        cast_w(0, 1, 2)
+        quant_w(0, 0, 1)
+        quant_w(0, 1, 2)
+        gather_words(1, 1, tag="w_grouped0_0")
+        cast_w(0, 2, 4)
+        cast_w(1, 0, 1)
+        quant_w(1, 0, 1)
+        cast_w(1, 1, 2)
+        quant_w(1, 1, 2)
+        quant_w(0, 2, 4, tag="w_grouped1_0")
+        make_h(0)
+        make_h(1)
+        cast_w(1, 2, 4)
+        quant_w(1, 2, 4)
+        make_h(2)
+        make_h(3)
+
+        sums = [bank(4 + vb, [P, PACK, P], f"sums{vb}") for vb in range(4)]
+        zT = [picked.tile([P, 2, P, 2], BF16, name=f"zT{vb}", tag=f"zT{vb}", align_bytes=64) for vb in range(4)]
+        back = [bank(b, [P, 2, 2 * P], f"back{b}") for b in range(2)]
+        z_grouped = picked.tile([P, V, 2], F32, tag="z_grouped", align_bytes=64)
+        slot = 0
+        for t in range(PACK):
+            for blocks in ((range(0, 2), range(2, 4)) if t == PACK - 1 else (range(0, 4),)):
+                for d in range(4):
+                    gt = picked.tile([P, len(blocks) * P], F32, name=f"nb{t}_{d}_{blocks.start}", tag=f"nb{slot % 8}", align_bytes=64)
+                    slot = slot + 1
+                    nc.vector.tensor_copy(gt[:], h[t][:].indirect(pos_t[d][:, 8 * blocks.start : 8 * blocks.stop]))
+                    for vb in blocks:
+                        nc.tensor.matmul(
+                            out=sums[vb][:, t, :],
+                            lhsT=gt[:, (vb - blocks.start) * P : (vb - blocks.start + 1) * P],
+                            rhs=ident[:],
+                            start=(d == 0),
+                            stop=(d == 3),
+                            is_transpose=True,
+                        )
+                if t % 2 == 1:
+                    u = t // 2
+                    for vb in blocks:
+                        nc.scalar.activation(
+                            zT[vb][:, u],
+                            sums[vb][:, 2 * u : 2 * u + 2, :].rearrange("v e p -> v p e"),
+                            COPY,
+                            scale=0.25,
+                        )
+                        nc.tensor.transpose(
+                            back[vb // 2][:, u, (vb % 2) * P : (vb % 2 + 1) * P],
+                            zT[vb][:, u].rearrange("v p e -> v (p e)").bitcast(F32),
+                            ident[:],
+                        )
+                if t == PACK - 1:
+                    b = blocks.start // 2
+                    nc.scalar.copy(z_grouped[:, b * 2 * P : (b + 1) * 2 * P, :], back[b][:].rearrange("p u v -> p v u"))
+
+        c_grouped = picked.tile([P, V, PACK], BF16, tag="zT3", align_bytes=64)
+
+        def gather_centres(piece, tag):
+            v0, v1 = PIECES[piece]
+            ct = picked.tile([P, PACK, v1 - v0], BF16, name=f"c_planes{piece}", tag=tag, align_bytes=64)
+            for t in range(PACK):
+                nc.vector.tensor_copy(ct[:, t, :], h[t][:].indirect(cen_t[:, v0 // 16 : v1 // 16]))
+            nc.scalar.copy(c_grouped[:, v0:v1, :], ct[:].rearrange("p t v -> p v t"))
+
+        gather_centres(0, f"nb{(slot - 4) % 8}")
+        gather_centres(1, f"nb{(slot - 3) % 8}")
+        z_words = keep.tile([P, V], U32, align_bytes=64)
+        z_bytes = keep.tile([P, V], U8, align_bytes=64)
+        nc.vector.quantize_mx(
+            out=z_words[:].bitcast(FP8X4),
+            scales=z_bytes[:],
+            in_=z_grouped[:].rearrange("p v u -> p (v u)").bitcast(BF16),
+        )
+        acc = {}
+        for piece, (v0, v1) in enumerate(PIECES):
+            for m in range(2):
+                acc[piece, m] = bank(2 + 2 * piece + m, [P, v1 - v0], f"o_acc{piece}_{m}")
+                nc.tensor.matmul_mx(
+                    out=acc[piece, m][:],
+                    lhsT=w23_words[1][:, m * P : (m + 1) * P].bitcast(FP8X4),
+                    lhsT_scale=w23_scales[:, N + m * P : N + (m + 1) * P],
+                    rhs=z_words[:, v0:v1].bitcast(FP8X4),
+                    rhs_scale=z_bytes[:, v0:v1],
+                    start=True,
+                    stop=False,
+                )
+        gather_centres(2, "z_grouped")
+        for piece, (v0, v1) in enumerate(PIECES):
+            cw = keep.tile([P, v1 - v0], U32, name=f"c_words{piece}", align_bytes=64)
+            cb = keep.tile([P, v1 - v0], U8, name=f"c_bytes{piece}", align_bytes=64)
+            nc.vector.quantize_mx(
+                out=cw[:].bitcast(FP8X4),
+                scales=cb[:],
+                in_=c_grouped[:, v0:v1, :].rearrange("p v t -> p (v t)"),
+            )
+            for m in range(2):
+                nc.tensor.matmul_mx(
+                    out=acc[piece, m][:],
+                    lhsT=w23_words[0][:, m * P : (m + 1) * P].bitcast(FP8X4),
+                    lhsT_scale=w23_scales[:, m * P : (m + 1) * P],
+                    rhs=cw[:].bitcast(FP8X4),
+                    rhs_scale=cb[:],
+                    start=False,
+                    stop=True,
+                )
+                res = keep.tile([P, v1 - v0], F32, name=f"res{piece}_{m}")
+                if m == 0:
+                    nc.vector.tensor_copy(res[:], acc[piece, m][:])
+                else:
+                    nc.scalar.copy(res[:], acc[piece, m][:])
+                nc.sync.dma_start(out[m * P : (m + 1) * P, v0:v1], res[:])

@@ -20,9 +20,9 @@ P = 128
 PACK = 4
 K_PASS = P * PACK
 BANK = 512
-X_CHUNKS = ((1024, 1024), (512, 512, 512, 256, 256))
+X_CHUNKS = ((1024, 512, 512), (512, 512, 512, 256, 256))
+SHARES = ((3, 3, 3), (0, 3, 4, 4, 5))
 UNIT = 512
-VECTOR_SHARE = 3
 PIECES = ((0, 256), (256, 384), (384, 512))
 
 
@@ -93,13 +93,17 @@ def tile_picked_sagecat_mean_e_kernel(
 
         for g in range(passes):
             c0 = 0
-            for n in X_CHUNKS[g]:
+            for n, share in zip(X_CHUNKS[g], SHARES[g]):
                 raw = x_raw[g, c0]
                 m = min(n, UNIT)
                 for u0 in range(0, n, m):
                     gt = ring.tile([P, m, PACK], BF16, name="x_grouped", align_bytes=64)
-                    cut = m * (5 if g == passes - 1 and c0 + n == T else VECTOR_SHARE) // 8
-                    nc.vector.tensor_copy(gt[:, :cut], raw[:, :, u0 : u0 + cut].rearrange("p j c -> p c j"))
+                    cut = m * share // 8
+                    if cut:
+                        nc.vector.tensor_copy(
+                            gt[:, :cut].rearrange("p (c i) j -> p c j i", i=4),
+                            raw[:, :, u0 : u0 + cut].rearrange("p j (c i) -> p c j i", i=4),
+                        )
                     nc.scalar.activation(
                         gt[:, cut:].rearrange("p (c i) j -> p c j i", i=4),
                         raw[:, :, u0 + cut : u0 + m].rearrange("p j (c i) -> p c j i", i=4),
@@ -121,11 +125,11 @@ def tile_picked_sagecat_mean_e_kernel(
 
         w_grouped, w_words, w_bytes = {}, {}, {}
 
-        def cast_w(g, t0, t1):
-            src = w_raw[g][:].rearrange("p j (m t) -> p m t j", t=PACK)
-            gt = picked.tile([P, t1 - t0, P, PACK], BF16, name=f"w_grouped{g}_{t0}", tag=f"w_grouped{g}_{t0}", align_bytes=64)
-            nc.scalar.activation(gt[:].rearrange("p t m j -> p m t j"), src[:, :, t0:t1, :], COPY)
-            w_grouped[g, t0] = gt
+        def cast_w(g, u):
+            src = w_raw[g][:].rearrange("p j (m t) -> p m j t", t=PACK)
+            gt = picked.tile([P, 2, P, PACK], BF16, name=f"w_grouped{g}_{u}", tag=f"w_grouped{g}_{u}", align_bytes=64)
+            nc.scalar.activation(gt[:].rearrange("p t m j -> p m j t"), src[:, :, :, 2 * u : 2 * u + 2], COPY)
+            w_grouped[g, u] = gt
 
         def quant_w(g, t0, t1, tag=None):
             n = (t1 - t0) * P
@@ -134,7 +138,7 @@ def tile_picked_sagecat_mean_e_kernel(
             nc.vector.quantize_mx(
                 out=words[:].bitcast(FP8X4),
                 scales=scales[:],
-                in_=w_grouped[g, t0][:].rearrange("p t m j -> p (t m j)"),
+                in_=w_grouped[g, t0 // 2][:, t0 % 2 : t0 % 2 + t1 - t0].rearrange("p t m j -> p (t m j)"),
             )
             for t in range(t0, t1):
                 w_words[g, t] = words[:, (t - t0) * P : (t - t0 + 1) * P]
@@ -144,43 +148,41 @@ def tile_picked_sagecat_mean_e_kernel(
 
         def make_h(t):
             ht = keep.tile([P, S], F32, name=f"h{t}")
-            acc = [bank(2 * (t // 2) + half, [P, BANK], f"h_acc{t}_{half}") for half in range(2)]
+            width = BANK // 2 if t == 0 else BANK
+            parts = range(S // width)
+            acc = [bank(2 * max(t - 1, 0) + part, [P, width], f"h_acc{t}_{part}") for part in parts]
             for g in range(passes):
-                for half in range(2):
+                for part in parts:
+                    half, c0 = divmod(part * width, BANK)
                     nc.tensor.matmul_mx(
-                        out=acc[half][:],
+                        out=acc[part][:],
                         lhsT=w_words[g, t].bitcast(FP8X4),
                         lhsT_scale=w_bytes[g, t],
-                        rhs=g_words[g, half][:].bitcast(FP8X4),
-                        rhs_scale=g_bytes[4 * g : P, half * BANK : (half + 1) * BANK],
+                        rhs=g_words[g, half][:, c0 : c0 + width].bitcast(FP8X4),
+                        rhs_scale=g_bytes[4 * g : P, part * width : (part + 1) * width],
                         start=(g == 0),
                         stop=(g == passes - 1),
                     )
-            for half in range(2):
-                dst = ht[:, half * BANK : (half + 1) * BANK]
-                if t == 0 and half == 1:
-                    nc.vector.tensor_scalar_max(dst, acc[half][:], 0.0)
+            for part in parts:
+                dst = ht[:, part * width : (part + 1) * width]
+                if t == 0 and part % 2 == 1:
+                    nc.vector.tensor_scalar_max(dst, acc[part][:], 0.0)
                 else:
-                    nc.scalar.activation(dst, acc[half][:], RELU)
+                    nc.scalar.activation(dst, acc[part][:], RELU)
             h[t] = ht
 
-        cast_w(0, 0, 1)
-        cast_w(0, 1, 2)
-        quant_w(0, 0, 1)
-        quant_w(0, 1, 2)
+        cast_w(0, 0)
+        quant_w(0, 0, 2)
         gather_words(1, 1, tag="w_grouped0_0")
-        cast_w(0, 2, 4)
-        cast_w(1, 0, 1)
+        cast_w(0, 1)
+        cast_w(1, 0)
         quant_w(1, 0, 1)
-        cast_w(1, 1, 2)
         quant_w(1, 1, 2)
         quant_w(0, 2, 4, tag="w_grouped1_0")
-        make_h(0)
-        make_h(1)
-        cast_w(1, 2, 4)
+        cast_w(1, 1)
         quant_w(1, 2, 4)
-        make_h(2)
-        make_h(3)
+        for t in range(PACK):
+            make_h(t)
 
         sums = [bank(4 + vb, [P, PACK, P], f"sums{vb}") for vb in range(4)]
         zT = [picked.tile([P, 2, P, 2], BF16, name=f"zT{vb}", tag=f"zT{vb}", align_bytes=64) for vb in range(4)]

@@ -21,7 +21,7 @@ PACK = 4
 K_PASS = P * PACK
 BANK = 512
 X_CHUNKS = ((1024, 512, 512), (512, 512, 512, 256, 256))
-SHARES = ((3, 3, 3), (0, 3, 4, 4, 5))
+SHARES = ((5, 5, 3), (0, 4, 4, 4, 5))
 UNIT = 512
 PIECES = ((0, 256), (256, 384), (384, 512))
 

@@ -23,6 +23,9 @@ BANK = 512
 X_CHUNKS = ((1024, 512, 512), (512, 512, 512, 256, 256))
 SHARES = ((5, 5, 3), (0, 4, 4, 4, 5))
 UNIT = 512
+QUARTER = 256
+ON_VECTOR = ((1, 1), (2, 1))
+H_BANKS = ((0, 1, 2, 3), (4, 5), (6, 7), (0, 1))
 PIECES = ((0, 256), (256, 384), (384, 512))
 
 
@@ -83,13 +86,18 @@ def tile_picked_sagecat_mean_e_kernel(
                     scales[0, 4 * q : 4 * q + 4, :].bitcast(I32),
                 )
 
-        x_words = [keep.tile([P, T], U32, name=f"x_words{g}", align_bytes=64) for g in range(passes)]
+        x_words = [picked.tile([P, T], U32, name=f"x_words{g}", tag=f"x_words{g}", align_bytes=64) for g in range(passes)]
         g_words = {}
 
-        def gather_words(g, half, tag=None):
-            t = picked.tile([P, BANK], U32, name=f"g_words{g}_{half}", tag=tag or f"g_words{g}_{half}", align_bytes=64)
-            nc.vector.tensor_copy(t[:], x_words[g][:].indirect(offs_t[:, half * 32 : (half + 1) * 32]))
-            g_words[g, half] = t
+        def gather_words(g, c0, n, tag=None, parts=1):
+            t = picked.tile([P, n], U32, name=f"g_words{g}_{c0}", tag=tag or f"g_words{g}_{c0}", align_bytes=64)
+            m = n // parts
+            for c in range(0, n, m):
+                nc.vector.tensor_copy(
+                    t[:, c : c + m], x_words[g][:].indirect(offs_t[:, (c0 + c) // 16 : (c0 + c + m) // 16])
+                )
+            for c in range(0, n, QUARTER):
+                g_words[g, c0 + c] = t[:, c:]
 
         for g in range(passes):
             c0 = 0
@@ -117,11 +125,9 @@ def tile_picked_sagecat_mean_e_kernel(
                     )
                 c0 = c0 + n
             if g == 0:
-                gather_words(0, 0)
-                gather_words(0, 1)
+                gather_words(0, 0, S)
         g_bytes = keep.tile([P, S], U8, align_bytes=64)
         nc.vector.tensor_copy(g_bytes[:], x_bytes[:].indirect(offs_t[:]))
-        gather_words(1, 0)
 
         w_grouped, w_words, w_bytes = {}, {}, {}
 
@@ -144,49 +150,59 @@ def tile_picked_sagecat_mean_e_kernel(
                 w_words[g, t] = words[:, (t - t0) * P : (t - t0 + 1) * P]
                 w_bytes[g, t] = scales[:, (t - t0) * P : (t - t0 + 1) * P]
 
-        h = {}
+        h, h_acc = {}, {}
 
-        def make_h(t):
-            ht = keep.tile([P, S], F32, name=f"h{t}")
-            width = BANK // 2 if t == 0 else BANK
-            parts = range(S // width)
-            acc = [bank(2 * max(t - 1, 0) + part, [P, width], f"h_acc{t}_{part}") for part in parts]
-            for g in range(passes):
-                for part in parts:
-                    half, c0 = divmod(part * width, BANK)
-                    nc.tensor.matmul_mx(
-                        out=acc[part][:],
-                        lhsT=w_words[g, t].bitcast(FP8X4),
-                        lhsT_scale=w_bytes[g, t],
-                        rhs=g_words[g, half][:, c0 : c0 + width].bitcast(FP8X4),
-                        rhs_scale=g_bytes[4 * g : P, part * width : (part + 1) * width],
-                        start=(g == 0),
-                        stop=(g == passes - 1),
-                    )
-            for part in parts:
+        def h_pass(t, g):
+            if g == 0:
+                h_acc[t] = [bank(b, [P, S // len(H_BANKS[t])], f"h_acc{t}_{b}") for b in H_BANKS[t]]
+            width = S // len(H_BANKS[t])
+            for part in range(len(H_BANKS[t])):
+                c0 = part * width
+                nc.tensor.matmul_mx(
+                    out=h_acc[t][part][:],
+                    lhsT=w_words[g, t].bitcast(FP8X4),
+                    lhsT_scale=w_bytes[g, t],
+                    rhs=g_words[g, c0][:, :width].bitcast(FP8X4),
+                    rhs_scale=g_bytes[4 * g : P, c0 : c0 + width],
+                    start=(g == 0),
+                    stop=(g == passes - 1),
+                )
+
+        def h_out(t, on_vector=()):
+            ht = picked.tile([P, S], F32, name=f"h{t}", tag=f"h{t}", align_bytes=64)
+            width = S // len(H_BANKS[t])
+            for part in range(len(H_BANKS[t])):
                 dst = ht[:, part * width : (part + 1) * width]
-                if t == 0 and part % 2 == 1:
-                    nc.vector.tensor_scalar_max(dst, acc[part][:], 0.0)
+                if part in on_vector:
+                    nc.vector.tensor_scalar_max(dst, h_acc[t][part][:], 0.0)
                 else:
-                    nc.scalar.activation(dst, acc[part][:], RELU)
+                    nc.scalar.activation(dst, h_acc[t][part][:], RELU)
             h[t] = ht
 
         cast_w(0, 0)
         quant_w(0, 0, 2)
-        gather_words(1, 1, tag="w_grouped0_0")
+        gather_words(1, 0, BANK, tag="w_grouped0_0")
         cast_w(0, 1)
         cast_w(1, 0)
-        quant_w(1, 0, 1)
-        quant_w(1, 1, 2)
-        quant_w(0, 2, 4, tag="w_grouped1_0")
+        quant_w(1, 0, 2)
+        gather_words(1, BANK, BANK, tag="w_grouped1_0", parts=2)
         cast_w(1, 1)
+        h_pass(0, 0)
+        h_pass(1, 0)
+        h_pass(0, 1)
+        quant_w(0, 2, 4, tag="x_words1")
         quant_w(1, 2, 4)
-        for t in range(PACK):
-            make_h(t)
+        h_out(0)
+        h_pass(1, 1)
+        h_out(1)
+        for t in range(2, PACK):
+            h_pass(t, 0)
+            h_pass(t, 1)
+            h_out(t)
 
         sums = [bank(4 + vb, [P, PACK, P], f"sums{vb}") for vb in range(4)]
         zT = [picked.tile([P, 2, P, 2], BF16, name=f"zT{vb}", tag=f"zT{vb}", align_bytes=64) for vb in range(4)]
-        back = [bank(b, [P, 2, 2 * P], f"back{b}") for b in range(2)]
+        back = [bank(2 + b, [P, 2, 2 * P], f"back{b}") for b in range(2)]
         z_grouped = picked.tile([P, V, 2], F32, tag="z_grouped", align_bytes=64)
         slot = 0
         for t in range(PACK):
@@ -222,59 +238,75 @@ def tile_picked_sagecat_mean_e_kernel(
                     b = blocks.start // 2
                     nc.scalar.copy(z_grouped[:, b * 2 * P : (b + 1) * 2 * P, :], back[b][:].rearrange("p u v -> p v u"))
 
-        c_grouped = picked.tile([P, V, PACK], BF16, tag="zT3", align_bytes=64)
+        c_grouped = []
+        c_first = picked.tile([P, PIECES[-1][0], PACK], BF16, tag="zT3", align_bytes=64)
 
         def gather_centres(piece, tag):
             v0, v1 = PIECES[piece]
             ct = picked.tile([P, PACK, v1 - v0], BF16, name=f"c_planes{piece}", tag=tag, align_bytes=64)
             for t in range(PACK):
                 nc.vector.tensor_copy(ct[:, t, :], h[t][:].indirect(cen_t[:, v0 // 16 : v1 // 16]))
-            nc.scalar.copy(c_grouped[:, v0:v1, :], ct[:].rearrange("p t v -> p v t"))
+            cg = c_first[:, v0:v1, :]
+            nc.scalar.copy(cg, ct[:].rearrange("p t v -> p v t"))
+            c_grouped.append(cg)
 
-        gather_centres(0, f"nb{(slot - 4) % 8}")
-        gather_centres(1, f"nb{(slot - 3) % 8}")
-        z_words = keep.tile([P, V], U32, align_bytes=64)
-        z_bytes = keep.tile([P, V], U8, align_bytes=64)
-        nc.vector.quantize_mx(
-            out=z_words[:].bitcast(FP8X4),
-            scales=z_bytes[:],
-            in_=z_grouped[:].rearrange("p v u -> p (v u)").bitcast(BF16),
-        )
+        def gather_last_centres(piece, tag):
+            v0, v1 = PIECES[piece]
+            both = picked.tile([P, 6 * (v1 - v0)], BF16, name=f"c_last{piece}", tag=tag, align_bytes=64)
+            ct = both[:, : 2 * (v1 - v0)].rearrange("p (t v) -> p t v", t=2)
+            cg = both[:, 2 * (v1 - v0) :].rearrange("p (v t) -> p v t", t=PACK)
+            for t in range(PACK):
+                dst = ct[:, t, :] if t < 2 else cg[:, :, t]
+                nc.vector.tensor_copy(dst, h[t][:].indirect(cen_t[:, v0 // 16 : v1 // 16]))
+            nc.scalar.copy(cg[:, :, 0:2], ct.rearrange("p t v -> p v t"))
+            c_grouped.append(cg)
+
+        def quantise(src, n, name, tag=None):
+            words = keep.tile([P, n], U32, name=f"{name}_words", align_bytes=64)
+            scales = picked.tile([P, n], U8, name=f"{name}_bytes", tag=tag or f"{name}_bytes", align_bytes=64)
+            nc.vector.quantize_mx(out=words[:].bitcast(FP8X4), scales=scales[:], in_=src)
+            return words, scales
+
+        def quantise_c(piece, tag=None):
+            v0, v1 = PIECES[piece]
+            return quantise(c_grouped[piece].rearrange("p v t -> p (v t)"), v1 - v0, f"c{piece}", tag)
+
         acc = {}
-        for piece, (v0, v1) in enumerate(PIECES):
-            for m in range(2):
-                acc[piece, m] = bank(2 + 2 * piece + m, [P, v1 - v0], f"o_acc{piece}_{m}")
-                nc.tensor.matmul_mx(
-                    out=acc[piece, m][:],
-                    lhsT=w23_words[1][:, m * P : (m + 1) * P].bitcast(FP8X4),
-                    lhsT_scale=w23_scales[:, N + m * P : N + (m + 1) * P],
-                    rhs=z_words[:, v0:v1].bitcast(FP8X4),
-                    rhs_scale=z_bytes[:, v0:v1],
-                    start=True,
-                    stop=False,
-                )
-        gather_centres(2, "z_grouped")
-        for piece, (v0, v1) in enumerate(PIECES):
-            cw = keep.tile([P, v1 - v0], U32, name=f"c_words{piece}", align_bytes=64)
-            cb = keep.tile([P, v1 - v0], U8, name=f"c_bytes{piece}", align_bytes=64)
-            nc.vector.quantize_mx(
-                out=cw[:].bitcast(FP8X4),
-                scales=cb[:],
-                in_=c_grouped[:, v0:v1, :].rearrange("p v t -> p (v t)"),
+
+        def product(piece, m, a, words, scales):
+            v0, v1 = PIECES[piece]
+            if a == 1:
+                acc[piece, m] = bank((0, 4, 6)[piece] + m, [P, v1 - v0], f"o_acc{piece}_{m}")
+            nc.tensor.matmul_mx(
+                out=acc[piece, m][:],
+                lhsT=w23_words[a][:, m * P : (m + 1) * P].bitcast(FP8X4),
+                lhsT_scale=w23_scales[:, a * N + m * P : a * N + (m + 1) * P],
+                rhs=words.bitcast(FP8X4),
+                rhs_scale=scales,
+                start=(a == 1),
+                stop=(a == 0),
             )
+
+        def finish(piece, words, scales):
+            v0, v1 = PIECES[piece]
             for m in range(2):
-                nc.tensor.matmul_mx(
-                    out=acc[piece, m][:],
-                    lhsT=w23_words[0][:, m * P : (m + 1) * P].bitcast(FP8X4),
-                    lhsT_scale=w23_scales[:, m * P : (m + 1) * P],
-                    rhs=cw[:].bitcast(FP8X4),
-                    rhs_scale=cb[:],
-                    start=False,
-                    stop=True,
-                )
+                product(piece, m, 0, words[:], scales[:])
                 res = keep.tile([P, v1 - v0], F32, name=f"res{piece}_{m}")
-                if m == 0:
+                if (piece, m) in ON_VECTOR:
                     nc.vector.tensor_copy(res[:], acc[piece, m][:])
                 else:
                     nc.scalar.copy(res[:], acc[piece, m][:])
                 nc.sync.dma_start(out[m * P : (m + 1) * P, v0:v1], res[:])
+
+        gather_centres(0, f"nb{(slot - 4) % 8}")
+        gather_centres(1, f"nb{(slot - 3) % 8}")
+        words, scales = quantise(z_grouped[:].rearrange("p v u -> p (v u)").bitcast(BF16), V, "z")
+        for piece, (v0, v1) in enumerate(PIECES):
+            for m in range(2):
+                product(piece, m, 1, words[:, v0:v1], scales[:, v0:v1])
+        first = quantise_c(0)
+        gather_last_centres(2, "z_grouped")
+        finish(0, *first)
+        finish(1, *quantise_c(1, "h2"))
+        cw, cb = quantise_c(2)
+        finish(2, cw, cb)

@@ -25,7 +25,7 @@ SHARES = ((5, 5, 3), (0, 4, 4, 4, 5))
 UNIT = 512
 QUARTER = 256
 ON_VECTOR = ((1, 1), (2, 1))
-H_BANKS = ((0, 1, 2, 3), (4, 5), (6, 7), (0, 1))
+H_BANKS = ((0, 1, 2, 3), (4, 5), (0, 1), (2, 3))
 PIECES = ((0, 256), (256, 384), (384, 512))
 
 
@@ -181,18 +181,18 @@ def tile_picked_sagecat_mean_e_kernel(
 
         cast_w(0, 0)
         quant_w(0, 0, 2)
-        gather_words(1, 0, BANK, tag="w_grouped0_0")
+        gather_words(1, 0, S, tag="w_grouped0_0")
         cast_w(0, 1)
         cast_w(1, 0)
-        quant_w(1, 0, 2)
-        gather_words(1, BANK, BANK, tag="w_grouped1_0", parts=2)
+        quant_w(1, 0, 1)
         cast_w(1, 1)
         h_pass(0, 0)
         h_pass(1, 0)
         h_pass(0, 1)
-        quant_w(0, 2, 4, tag="x_words1")
+        quant_w(1, 1, 2)
+        quant_w(0, 2, 4, tag="w_grouped1_0")
+        h_out(0, (1, 3))
         quant_w(1, 2, 4)
-        h_out(0)
         h_pass(1, 1)
         h_out(1)
         for t in range(2, PACK):
@@ -200,9 +200,9 @@ def tile_picked_sagecat_mean_e_kernel(
             h_pass(t, 1)
             h_out(t)
 
-        sums = [bank(4 + vb, [P, PACK, P], f"sums{vb}") for vb in range(4)]
+        sums = [bank((2, 3, 6, 7)[vb], [P, PACK, P], f"sums{vb}") for vb in range(4)]
         zT = [picked.tile([P, 2, P, 2], BF16, name=f"zT{vb}", tag=f"zT{vb}", align_bytes=64) for vb in range(4)]
-        back = [bank(2 + b, [P, 2, 2 * P], f"back{b}") for b in range(2)]
+        back = [bank(4 + b, [P, 2, 2 * P], f"back{b}") for b in range(2)]
         z_grouped = picked.tile([P, V, 2], F32, tag="z_grouped", align_bytes=64)
         slot = 0
         for t in range(PACK):
@@ -276,7 +276,7 @@ def tile_picked_sagecat_mean_e_kernel(
         def product(piece, m, a, words, scales):
             v0, v1 = PIECES[piece]
             if a == 1:
-                acc[piece, m] = bank((0, 4, 6)[piece] + m, [P, v1 - v0], f"o_acc{piece}_{m}")
+                acc[piece, m] = bank((0, 2, 6)[piece] + m, [P, v1 - v0], f"o_acc{piece}_{m}")
             nc.tensor.matmul_mx(
                 out=acc[piece, m][:],
                 lhsT=w23_words[a][:, m * P : (m + 1) * P].bitcast(FP8X4),

@@ -24,7 +24,7 @@ X_CHUNKS = ((1024, 512, 512), (512, 512, 512, 256, 256))
 SHARES = ((5, 5, 3), (0, 4, 4, 4, 5))
 UNIT = 512
 QUARTER = 256
-ON_VECTOR = ((1, 1), (2, 1))
+ON_VECTOR = ((0, 0), (2, 1))
 H_BANKS = ((0, 1, 2, 3), (4, 5), (0, 1), (2, 3))
 PIECES = ((0, 256), (256, 384), (384, 512))
 
@@ -252,14 +252,10 @@ def tile_picked_sagecat_mean_e_kernel(
 
         def gather_last_centres(piece, tag):
             v0, v1 = PIECES[piece]
-            both = picked.tile([P, 6 * (v1 - v0)], BF16, name=f"c_last{piece}", tag=tag, align_bytes=64)
-            ct = both[:, : 2 * (v1 - v0)].rearrange("p (t v) -> p t v", t=2)
-            cg = both[:, 2 * (v1 - v0) :].rearrange("p (v t) -> p v t", t=PACK)
+            ct = picked.tile([P, PACK, v1 - v0], BF16, name=f"c_planes{piece}", tag=tag, align_bytes=64)
             for t in range(PACK):
-                dst = ct[:, t, :] if t < 2 else cg[:, :, t]
-                nc.vector.tensor_copy(dst, h[t][:].indirect(cen_t[:, v0 // 16 : v1 // 16]))
-            nc.scalar.copy(cg[:, :, 0:2], ct.rearrange("p t v -> p v t"))
-            c_grouped.append(cg)
+                nc.vector.tensor_copy(ct[:, t, :], h[t][:].indirect(cen_t[:, v0 // 16 : v1 // 16]))
+            return ct
 
         def quantise(src, n, name, tag=None):
             words = keep.tile([P, n], U32, name=f"{name}_words", align_bytes=64)
@@ -305,8 +301,14 @@ def tile_picked_sagecat_mean_e_kernel(
             for m in range(2):
                 product(piece, m, 1, words[:, v0:v1], scales[:, v0:v1])
         first = quantise_c(0)
-        gather_last_centres(2, "z_grouped")
+        ct = gather_last_centres(2, "z_grouped")
+        second = quantise_c(1, "h2")
+        cg = keep.tile([P, P, PACK], BF16, name="c_last", align_bytes=64)
+        nc.vector.tensor_copy(
+            cg[:].rearrange("p (c i) t -> p c t i", i=4), ct[:].rearrange("p t (c i) -> p c t i", i=4)
+        )
+        c_grouped.append(cg[:])
         finish(0, *first)
-        finish(1, *quantise_c(1, "h2"))
+        finish(1, *second)
         cw, cb = quantise_c(2)
         finish(2, cw, cb)

@@ -206,8 +206,9 @@ def tile_picked_sagecat_mean_e_kernel(
         z_grouped = picked.tile([P, V, 2], F32, tag="z_grouped", align_bytes=64)
         slot = 0
         for t in range(PACK):
-            for blocks in ((range(0, 2), range(2, 4)) if t == PACK - 1 else (range(0, 4),)):
-                for d in range(4):
+            for d in range(4):
+                last = (t, d) == (PACK - 1, 3)
+                for blocks in (range(0, 2), range(2, 4)) if last else (range(0, 4),):
                     gt = picked.tile([P, len(blocks) * P], F32, name=f"nb{t}_{d}_{blocks.start}", tag=f"nb{slot % 8}", align_bytes=64)
                     slot = slot + 1
                     nc.vector.tensor_copy(gt[:], h[t][:].indirect(pos_t[d][:, 8 * blocks.start : 8 * blocks.stop]))
@@ -220,35 +221,38 @@ def tile_picked_sagecat_mean_e_kernel(
                             stop=(d == 3),
                             is_transpose=True,
                         )
-                if t % 2 == 1:
-                    u = t // 2
-                    for vb in blocks:
-                        nc.scalar.activation(
-                            zT[vb][:, u],
-                            sums[vb][:, 2 * u : 2 * u + 2, :].rearrange("v e p -> v p e"),
-                            COPY,
-                            scale=0.25,
-                        )
-                        nc.tensor.transpose(
-                            back[vb // 2][:, u, (vb % 2) * P : (vb % 2 + 1) * P],
-                            zT[vb][:, u].rearrange("v p e -> v (p e)").bitcast(F32),
-                            ident[:],
-                        )
-                if t == PACK - 1:
-                    b = blocks.start // 2
-                    nc.scalar.copy(z_grouped[:, b * 2 * P : (b + 1) * 2 * P, :], back[b][:].rearrange("p u v -> p v u"))
+                    if t % 2 == 1 and d == 3:
+                        u = t // 2
+                        for vb in blocks:
+                            nc.scalar.activation(
+                                zT[vb][:, u],
+                                sums[vb][:, 2 * u : 2 * u + 2, :].rearrange("v e p -> v p e"),
+                                COPY,
+                                scale=0.25,
+                            )
+                            nc.tensor.transpose(
+                                back[vb // 2][:, u, (vb % 2) * P : (vb % 2 + 1) * P],
+                                zT[vb][:, u].rearrange("v p e -> v (p e)").bitcast(F32),
+                                ident[:],
+                            )
+                    if last:
+                        b = blocks.start // 2
+                        nc.scalar.copy(z_grouped[:, b * 2 * P : (b + 1) * 2 * P, :], back[b][:].rearrange("p u v -> p v u"))
 
         c_grouped = []
         c_first = picked.tile([P, PIECES[-1][0], PACK], BF16, tag="zT3", align_bytes=64)
 
-        def gather_centres(piece, tag):
-            v0, v1 = PIECES[piece]
-            ct = picked.tile([P, PACK, v1 - v0], BF16, name=f"c_planes{piece}", tag=tag, align_bytes=64)
-            for t in range(PACK):
-                nc.vector.tensor_copy(ct[:, t, :], h[t][:].indirect(cen_t[:, v0 // 16 : v1 // 16]))
-            cg = c_first[:, v0:v1, :]
-            nc.scalar.copy(cg, ct[:].rearrange("p t v -> p v t"))
-            c_grouped.append(cg)
+        def gather_first_centres(tag):
+            n = PIECES[-1][0]
+            ct = picked.tile([P, PACK, n], BF16, name="c_planes", tag=tag, align_bytes=64)
+            for t in range(PACK - 1):
+                nc.vector.tensor_copy(ct[:, t, :], h[t][:].indirect(cen_t[:, : n // 16]))
+            for v0, v1 in PIECES[:-1]:
+                nc.vector.tensor_copy(ct[:, PACK - 1, v0:v1], h[PACK - 1][:].indirect(cen_t[:, v0 // 16 : v1 // 16]))
+            for v0, v1 in PIECES[:-1]:
+                cg = c_first[:, v0:v1, :]
+                nc.scalar.copy(cg, ct[:, :, v0:v1].rearrange("p t v -> p v t"))
+                c_grouped.append(cg)
 
         def gather_last_centres(piece, tag):
             v0, v1 = PIECES[piece]
@@ -294,8 +298,7 @@ def tile_picked_sagecat_mean_e_kernel(
                     nc.scalar.copy(res[:], acc[piece, m][:])
                 nc.sync.dma_start(out[m * P : (m + 1) * P, v0:v1], res[:])
 
-        gather_centres(0, f"nb{(slot - 4) % 8}")
-        gather_centres(1, f"nb{(slot - 3) % 8}")
+        gather_first_centres(f"nb{(slot - 3) % 8}")
         words, scales = quantise(z_grouped[:].rearrange("p v u -> p (v u)").bitcast(BF16), V, "z")
         for piece, (v0, v1) in enumerate(PIECES):
             for m in range(2):

@@ -19,14 +19,16 @@ RELU = mybir.ActivationFunctionType.Relu
 P = 128
 PACK = 4
 K_PASS = P * PACK
-BANK = 512
-X_CHUNKS = ((1024, 512, 512), (512, 512, 512, 256, 256))
-SHARES = ((5, 5, 3), (0, 4, 4, 4, 5))
-UNIT = 512
-QUARTER = 256
-ON_VECTOR = ((0, 0), (2, 1))
-H_BANKS = ((0, 1, 2, 3), (4, 5), (0, 1), (2, 3))
+
+VEC, SCA = "vector", "scalar"
+PLANE_CUT = 384
+LAST_PLANE = ((VEC, 0, 256), (SCA, 256, 512), (SCA, 512, 768), (SCA, 768, 1024))
+H_BANKS = ((0, 1, 2, 3), (4, 5), (0, 1), (4, 5))
+SUM_BANKS = (2, 3, 6, 7)
+NEIGHBOURS = ((VEC, 0, 0, 4), (SCA, 2, 0, 4), (VEC, 1, 0, 4), (SCA, 3, 3, 4), (VEC, 3, 0, 3))
+RING = 10
 PIECES = ((0, 256), (256, 384), (384, 512))
+OUT_BANKS = (4, 2, 6)
 
 
 def tile_picked_sagecat_mean_e_kernel(
@@ -36,8 +38,7 @@ def tile_picked_sagecat_mean_e_kernel(
     passes = K // K_PASS
     with ExitStack() as ctx:
         keep = ctx.enter_context(tc.tile_pool(name="keep", bufs=1))
-        ring = ctx.enter_context(tc.tile_pool(name="ring", bufs=4))
-        picked = ctx.enter_context(tc.tile_pool(name="picked", bufs=1))
+        work = ctx.enter_context(tc.tile_pool(name="work", bufs=1))
         psum = ctx.enter_context(tc.psum_pool(name="psum", bufs=1))
 
         def bank(b, shape, name):
@@ -48,25 +49,38 @@ def tile_picked_sagecat_mean_e_kernel(
             nc.sync.dma_start(t[:], src)
             return t
 
-        x_bytes = keep.tile([P, T], U8, align_bytes=64)
-        nc.vector.memset(x_bytes[:].bitcast(I32), 0)
+        def gather(engine, dst, window, offsets):
+            if engine == VEC:
+                nc.vector.tensor_copy(dst, window[:].indirect(offsets))
+            else:
+                nc.scalar.activation(dst, window[:].indirect(offsets), COPY)
+
+        def interleave(engine, dst, src):
+            views = (dst.rearrange("p (c i) j -> p c j i", i=4), src.rearrange("p j (c i) -> p c j i", i=4))
+            if engine == VEC:
+                nc.vector.tensor_copy(*views)
+            else:
+                nc.scalar.copy(*views)
+
+        def quantise(src, n, name, tag=None):
+            words = keep.tile([P, n], U32, name=f"{name}_words", align_bytes=64)
+            scales = work.tile([P, n], U8, name=f"{name}_scales", tag=tag or f"{name}_scales", align_bytes=64)
+            nc.vector.quantize_mx(out=words[:].bitcast(FP8X4), scales=scales[:], in_=src)
+            return words, scales
+
         w23_scales = keep.tile([P, 2 * N], U8, align_bytes=64)
         nc.vector.memset(w23_scales[:].bitcast(I32), 0)
         ident = keep.tile([P, P], F32)
         make_identity(nc, ident[:])
 
+        offs_t = load_list(offs, "offs_t")
         x_raw = {}
-        offs_t = None
         for g in range(passes):
             rows = xT[g * K_PASS : (g + 1) * K_PASS, :].rearrange("(p j) c -> p j c", j=PACK)
-            c0 = 0
-            for n in X_CHUNKS[g]:
-                raw = keep.tile([P, PACK, n], F32, name=f"x_raw_{g}_{c0}")
-                nc.sync.dma_start(raw[:], rows[:, :, c0 : c0 + n])
-                x_raw[g, c0] = raw
-                c0 = c0 + n
-            if g == 0:
-                offs_t = load_list(offs, "offs_t")
+            for j in range(PACK):
+                raw = keep.tile([P, T], F32, name=f"x_raw_{g}_{j}")
+                nc.sync.dma_start(raw[:], rows[:, j, :])
+                x_raw[g, j] = raw
         w_raw = []
         for g in range(passes):
             raw = keep.tile([P, PACK, H], F32, name=f"w_raw_{g}")
@@ -75,101 +89,90 @@ def tile_picked_sagecat_mean_e_kernel(
         pos_t = [load_list(src, f"pos_t{d}") for d, src in enumerate((pos1, pos2, pos3, pos4))]
         cen_t = load_list(cen, "cen_t")
         w23_words = []
-        for a, (words, scales) in enumerate(((w2_words, w2_scales), (w3_words, w3_scales))):
+        for a, words in enumerate((w2_words, w3_words)):
             wt = keep.tile([P, N], I32, name=f"w23_words{a}", align_bytes=64)
             nc.sync.dma_start(wt[:], words[0].rearrange("p n t -> p (n t)").bitcast(I32))
             w23_words.append(wt)
-        for a, (words, scales) in enumerate(((w2_words, w2_scales), (w3_words, w3_scales))):
+        for a, scales in enumerate((w2_scales, w3_scales)):
             for q in range(4):
                 nc.sync.dma_start(
                     w23_scales[32 * q : 32 * q + 4, a * N : (a + 1) * N].bitcast(I32),
                     scales[0, 4 * q : 4 * q + 4, :].bitcast(I32),
                 )
 
-        x_words = [picked.tile([P, T], U32, name=f"x_words{g}", tag=f"x_words{g}", align_bytes=64) for g in range(passes)]
-        g_words = {}
+        planes = [keep.tile([P, PACK, S], BF16, name=f"planes{g}", align_bytes=64) for g in range(passes)]
+        x_words = [keep.tile([P, S], U32, name=f"x_words{g}", align_bytes=64) for g in range(passes)]
+        x_scales = {}
+        x_grouped = {}
 
-        def gather_words(g, c0, n, tag=None, parts=1):
-            t = picked.tile([P, n], U32, name=f"g_words{g}_{c0}", tag=tag or f"g_words{g}_{c0}", align_bytes=64)
-            m = n // parts
-            for c in range(0, n, m):
-                nc.vector.tensor_copy(
-                    t[:, c : c + m], x_words[g][:].indirect(offs_t[:, (c0 + c) // 16 : (c0 + c + m) // 16])
-                )
-            for c in range(0, n, QUARTER):
-                g_words[g, c0 + c] = t[:, c:]
+        def gather_plane(g, j, cuts=((VEC, 0, PLANE_CUT), (SCA, PLANE_CUT, S))):
+            for engine, c0, c1 in cuts:
+                gather(engine, planes[g][:, j, c0:c1], x_raw[g, j], offs_t[:, c0 // 16 : c1 // 16])
 
-        for g in range(passes):
-            c0 = 0
-            for n, share in zip(X_CHUNKS[g], SHARES[g]):
-                raw = x_raw[g, c0]
-                m = min(n, UNIT)
-                for u0 in range(0, n, m):
-                    gt = ring.tile([P, m, PACK], BF16, name="x_grouped", align_bytes=64)
-                    cut = m * share // 8
-                    if cut:
-                        nc.vector.tensor_copy(
-                            gt[:, :cut].rearrange("p (c i) j -> p c j i", i=4),
-                            raw[:, :, u0 : u0 + cut].rearrange("p j (c i) -> p c j i", i=4),
-                        )
-                    nc.scalar.activation(
-                        gt[:, cut:].rearrange("p (c i) j -> p c j i", i=4),
-                        raw[:, :, u0 + cut : u0 + m].rearrange("p j (c i) -> p c j i", i=4),
-                        COPY,
-                    )
-                    cols = slice(c0 + u0, c0 + u0 + m)
-                    nc.vector.quantize_mx(
-                        out=x_words[g][:, cols].bitcast(FP8X4),
-                        scales=x_bytes[4 * g : P, cols],
-                        in_=gt[:].rearrange("p c j -> p (c j)"),
-                    )
-                c0 = c0 + n
-            if g == 0:
-                gather_words(0, 0, S)
-        g_bytes = keep.tile([P, S], U8, align_bytes=64)
-        nc.vector.tensor_copy(g_bytes[:], x_bytes[:].indirect(offs_t[:]))
+        def group_x(engine, g, c0, c1):
+            half = c0 // 512
+            if (g, half) not in x_grouped:
+                x_grouped[g, half] = keep.tile([P, 512, PACK], BF16, name=f"x_grouped{g}_{half}", align_bytes=64)
+            interleave(engine, x_grouped[g, half][:, c0 % 512 : c0 % 512 + c1 - c0, :], planes[g][:, :, c0:c1])
 
-        w_grouped, w_words, w_bytes = {}, {}, {}
-
-        def cast_w(g, u):
-            src = w_raw[g][:].rearrange("p j (m t) -> p m j t", t=PACK)
-            gt = picked.tile([P, 2, P, PACK], BF16, name=f"w_grouped{g}_{u}", tag=f"w_grouped{g}_{u}", align_bytes=64)
-            nc.scalar.activation(gt[:].rearrange("p t m j -> p m j t"), src[:, :, :, 2 * u : 2 * u + 2], COPY)
-            w_grouped[g, u] = gt
-
-        def quant_w(g, t0, t1, tag=None):
-            n = (t1 - t0) * P
-            words = keep.tile([P, n], U32, name=f"w_words{g}_{t0}", align_bytes=64)
-            scales = picked.tile([P, n], U8, name=f"w_bytes{g}_{t0}", tag=tag or f"w_bytes{g}_{t0}", align_bytes=64)
+        def quantise_x(g, c0, c1, tag=None):
+            if g not in x_scales:
+                x_scales[g] = work.tile([P, S], U8, name=f"x_scales{g}", tag=tag or f"x_scales{g}", align_bytes=64)
             nc.vector.quantize_mx(
-                out=words[:].bitcast(FP8X4),
-                scales=scales[:],
-                in_=w_grouped[g, t0 // 2][:, t0 % 2 : t0 % 2 + t1 - t0].rearrange("p t m j -> p (t m j)"),
+                out=x_words[g][:, c0:c1].bitcast(FP8X4),
+                scales=x_scales[g][:, c0:c1],
+                in_=x_grouped[g, c0 // 512][:, c0 % 512 : c0 % 512 + c1 - c0, :].rearrange("p c j -> p (c j)"),
             )
+
+        for j in range(PACK):
+            gather_plane(0, j)
+        gather_plane(1, 0)
+        group_x(VEC, 0, 0, 512)
+        gather_plane(1, 1)
+        quantise_x(0, 0, 512)
+        group_x(VEC, 0, 512, 1024)
+        gather_plane(1, 2)
+        quantise_x(0, 512, 1024)
+        gather_plane(1, 3, LAST_PLANE)
+        w_grouped, w_words, w_scales = {}, {}, {}
+
+        def cast_w(engine, g, u, m0=0, m1=P):
+            if (g, u) not in w_grouped:
+                w_grouped[g, u] = work.tile([P, 2, P, PACK], BF16, name=f"w_grouped{g}_{u}", tag=f"w_grouped{g}_{u}", align_bytes=64)
+            src = w_raw[g][:].rearrange("p j (m t) -> p m j t", t=PACK)[:, m0:m1, :, 2 * u : 2 * u + 2]
+            dst = w_grouped[g, u][:, :, m0:m1, :].rearrange("p t m j -> p m j t")
+            if engine == VEC:
+                nc.vector.tensor_copy(dst, src)
+            else:
+                nc.scalar.activation(dst, src, COPY)
+
+        def quantise_w(g, t0, t1):
+            src = w_grouped[g, t0 // 2][:, t0 % 2 : t0 % 2 + t1 - t0].rearrange("p t m j -> p (t m j)")
+            words, scales = quantise(src, (t1 - t0) * P, f"w{g}_{t0}")
             for t in range(t0, t1):
                 w_words[g, t] = words[:, (t - t0) * P : (t - t0 + 1) * P]
-                w_bytes[g, t] = scales[:, (t - t0) * P : (t - t0 + 1) * P]
+                w_scales[g, t] = scales[:, (t - t0) * P : (t - t0 + 1) * P]
 
         h, h_acc = {}, {}
 
         def h_pass(t, g):
-            if g == 0:
-                h_acc[t] = [bank(b, [P, S // len(H_BANKS[t])], f"h_acc{t}_{b}") for b in H_BANKS[t]]
             width = S // len(H_BANKS[t])
+            if g == 0:
+                h_acc[t] = [bank(b, [P, width], f"h_acc{t}_{b}") for b in H_BANKS[t]]
             for part in range(len(H_BANKS[t])):
-                c0 = part * width
+                cols = slice(part * width, (part + 1) * width)
                 nc.tensor.matmul_mx(
                     out=h_acc[t][part][:],
                     lhsT=w_words[g, t].bitcast(FP8X4),
-                    lhsT_scale=w_bytes[g, t],
-                    rhs=g_words[g, c0][:, :width].bitcast(FP8X4),
-                    rhs_scale=g_bytes[4 * g : P, c0 : c0 + width],
+                    lhsT_scale=w_scales[g, t],
+                    rhs=x_words[g][:, cols].bitcast(FP8X4),
+                    rhs_scale=x_scales[g][:, cols],
                     start=(g == 0),
                     stop=(g == passes - 1),
                 )
 
         def h_out(t, on_vector=()):
-            ht = picked.tile([P, S], F32, name=f"h{t}", tag=f"h{t}", align_bytes=64)
+            ht = keep.tile([P, S], F32, name=f"h{t}", align_bytes=64)
             width = S // len(H_BANKS[t])
             for part in range(len(H_BANKS[t])):
                 dst = ht[:, part * width : (part + 1) * width]
@@ -179,20 +182,25 @@ def tile_picked_sagecat_mean_e_kernel(
                     nc.scalar.activation(dst, h_acc[t][part][:], RELU)
             h[t] = ht
 
-        cast_w(0, 0)
-        quant_w(0, 0, 2)
-        gather_words(1, 0, S, tag="w_grouped0_0")
-        cast_w(0, 1)
-        cast_w(1, 0)
-        quant_w(1, 0, 1)
-        cast_w(1, 1)
+        cast_w(SCA, 0, 0)
+        cast_w(SCA, 0, 1)
+        quantise_w(0, 0, 2)
+        group_x(VEC, 1, 256, 512)
+        group_x(VEC, 1, 0, 256)
+        group_x(VEC, 1, 512, 768)
+        group_x(VEC, 1, 768, 1024)
+        quantise_x(1, 0, 512, tag="w_grouped0_0")
+        quantise_x(1, 512, 1024)
         h_pass(0, 0)
         h_pass(1, 0)
+        cast_w(SCA, 1, 0)
+        quantise_w(1, 0, 1)
+        cast_w(SCA, 1, 1)
+        quantise_w(1, 1, 2)
+        quantise_w(0, 2, 4)
         h_pass(0, 1)
-        quant_w(1, 1, 2)
-        quant_w(0, 2, 4, tag="w_grouped1_0")
         h_out(0, (1, 3))
-        quant_w(1, 2, 4)
+        quantise_w(1, 2, 4)
         h_pass(1, 1)
         h_out(1)
         for t in range(2, PACK):
@@ -200,83 +208,62 @@ def tile_picked_sagecat_mean_e_kernel(
             h_pass(t, 1)
             h_out(t)
 
-        sums = [bank((2, 3, 6, 7)[vb], [P, PACK, P], f"sums{vb}") for vb in range(4)]
-        zT = [picked.tile([P, 2, P, 2], BF16, name=f"zT{vb}", tag=f"zT{vb}", align_bytes=64) for vb in range(4)]
-        back = [bank(4 + b, [P, 2, 2 * P], f"back{b}") for b in range(2)]
-        z_grouped = picked.tile([P, V, 2], F32, tag="z_grouped", align_bytes=64)
+        sums = [bank(b, [P, PACK, P], f"sums{vb}") for vb, b in enumerate(SUM_BANKS)]
+        zT = [keep.tile([P, 2, P, 2], BF16, name=f"zT{vb}", align_bytes=64) for vb in range(4)]
+        back = [bank(b, [P, 2, 2 * P], f"back{b}") for b in range(2)]
+        z_grouped = keep.tile([P, V, 2], F32, align_bytes=64)
         slot = 0
         for t in range(PACK):
-            for d in range(4):
-                last = (t, d) == (PACK - 1, 3)
-                for blocks in (range(0, 2), range(2, 4)) if last else (range(0, 4),):
-                    gt = picked.tile([P, len(blocks) * P], F32, name=f"nb{t}_{d}_{blocks.start}", tag=f"nb{slot % 8}", align_bytes=64)
-                    slot = slot + 1
-                    nc.vector.tensor_copy(gt[:], h[t][:].indirect(pos_t[d][:, 8 * blocks.start : 8 * blocks.stop]))
-                    for vb in blocks:
-                        nc.tensor.matmul(
-                            out=sums[vb][:, t, :],
-                            lhsT=gt[:, (vb - blocks.start) * P : (vb - blocks.start + 1) * P],
-                            rhs=ident[:],
-                            start=(d == 0),
-                            stop=(d == 3),
-                            is_transpose=True,
-                        )
-                    if t % 2 == 1 and d == 3:
+            added = [0] * 4
+            for engine, d, b0, b1 in NEIGHBOURS:
+                gt = work.tile([P, (b1 - b0) * P], F32, name=f"nb{t}_{d}_{b0}", tag=f"nb{slot % RING}", align_bytes=64)
+                slot = slot + 1
+                gather(engine, gt[:], h[t], pos_t[d][:, 8 * b0 : 8 * b1])
+                for vb in range(b0, b1):
+                    nc.tensor.matmul(
+                        out=sums[vb][:, t, :],
+                        lhsT=gt[:, (vb - b0) * P : (vb - b0 + 1) * P],
+                        rhs=ident[:],
+                        start=(added[vb] == 0),
+                        stop=(added[vb] == 3),
+                        is_transpose=True,
+                    )
+                    added[vb] = added[vb] + 1
+                    if t % 2 == 1 and added[vb] == 4:
                         u = t // 2
-                        for vb in blocks:
-                            nc.scalar.activation(
-                                zT[vb][:, u],
-                                sums[vb][:, 2 * u : 2 * u + 2, :].rearrange("v e p -> v p e"),
-                                COPY,
-                                scale=0.25,
-                            )
-                            nc.tensor.transpose(
-                                back[vb // 2][:, u, (vb % 2) * P : (vb % 2 + 1) * P],
-                                zT[vb][:, u].rearrange("v p e -> v (p e)").bitcast(F32),
-                                ident[:],
-                            )
-                    if last:
-                        b = blocks.start // 2
-                        nc.scalar.copy(z_grouped[:, b * 2 * P : (b + 1) * 2 * P, :], back[b][:].rearrange("p u v -> p v u"))
+                        nc.scalar.activation(
+                            zT[vb][:, u],
+                            sums[vb][:, 2 * u : 2 * u + 2, :].rearrange("v e p -> v p e"),
+                            COPY,
+                            scale=0.25,
+                        )
+                        nc.tensor.transpose(
+                            back[vb // 2][:, u, (vb % 2) * P : (vb % 2 + 1) * P],
+                            zT[vb][:, u].rearrange("v p e -> v (p e)").bitcast(F32),
+                            ident[:],
+                        )
+                        if u == 1 and added[vb ^ 1] == 4:
+                            b = vb // 2
+                            nc.scalar.copy(z_grouped[:, b * 2 * P : (b + 1) * 2 * P, :], back[b][:].rearrange("p u v -> p v u"))
 
-        c_grouped = []
-        c_first = picked.tile([P, PIECES[-1][0], PACK], BF16, tag="zT3", align_bytes=64)
-
-        def gather_first_centres(tag):
-            n = PIECES[-1][0]
-            ct = picked.tile([P, PACK, n], BF16, name="c_planes", tag=tag, align_bytes=64)
-            for t in range(PACK - 1):
-                nc.vector.tensor_copy(ct[:, t, :], h[t][:].indirect(cen_t[:, : n // 16]))
-            for v0, v1 in PIECES[:-1]:
-                nc.vector.tensor_copy(ct[:, PACK - 1, v0:v1], h[PACK - 1][:].indirect(cen_t[:, v0 // 16 : v1 // 16]))
-            for v0, v1 in PIECES[:-1]:
-                cg = c_first[:, v0:v1, :]
-                nc.scalar.copy(cg, ct[:, :, v0:v1].rearrange("p t v -> p v t"))
-                c_grouped.append(cg)
-
-        def gather_last_centres(piece, tag):
+        def gather_centres(piece, tag):
             v0, v1 = PIECES[piece]
-            ct = picked.tile([P, PACK, v1 - v0], BF16, name=f"c_planes{piece}", tag=tag, align_bytes=64)
+            ct = work.tile([P, PACK, v1 - v0], BF16, name=f"c_planes{piece}", tag=tag, align_bytes=64)
             for t in range(PACK):
-                nc.vector.tensor_copy(ct[:, t, :], h[t][:].indirect(cen_t[:, v0 // 16 : v1 // 16]))
+                gather((VEC, SCA)[t % 2], ct[:, t, :], h[t], cen_t[:, v0 // 16 : v1 // 16])
             return ct
 
-        def quantise(src, n, name, tag=None):
-            words = keep.tile([P, n], U32, name=f"{name}_words", align_bytes=64)
-            scales = picked.tile([P, n], U8, name=f"{name}_bytes", tag=tag or f"{name}_bytes", align_bytes=64)
-            nc.vector.quantize_mx(out=words[:].bitcast(FP8X4), scales=scales[:], in_=src)
-            return words, scales
-
-        def quantise_c(piece, tag=None):
-            v0, v1 = PIECES[piece]
-            return quantise(c_grouped[piece].rearrange("p v t -> p (v t)"), v1 - v0, f"c{piece}", tag)
+        def group_centres(piece, ct):
+            cg = keep.tile([P, ct.shape[2], PACK], BF16, name=f"c_grouped{piece}", align_bytes=64)
+            interleave(VEC, cg[:], ct[:])
+            return cg
 
         acc = {}
 
         def product(piece, m, a, words, scales):
             v0, v1 = PIECES[piece]
             if a == 1:
-                acc[piece, m] = bank((0, 2, 6)[piece] + m, [P, v1 - v0], f"o_acc{piece}_{m}")
+                acc[piece, m] = bank(OUT_BANKS[piece] + m, [P, v1 - v0], f"o_acc{piece}_{m}")
             nc.tensor.matmul_mx(
                 out=acc[piece, m][:],
                 lhsT=w23_words[a][:, m * P : (m + 1) * P].bitcast(FP8X4),
@@ -287,31 +274,26 @@ def tile_picked_sagecat_mean_e_kernel(
                 stop=(a == 0),
             )
 
-        def finish(piece, words, scales):
+        def finish(piece, cg):
             v0, v1 = PIECES[piece]
+            words, scales = quantise(cg[:].rearrange("p v t -> p (v t)"), v1 - v0, f"c{piece}")
             for m in range(2):
                 product(piece, m, 0, words[:], scales[:])
                 res = keep.tile([P, v1 - v0], F32, name=f"res{piece}_{m}")
-                if (piece, m) in ON_VECTOR:
+                if (piece, m) == (2, 1):
                     nc.vector.tensor_copy(res[:], acc[piece, m][:])
                 else:
                     nc.scalar.copy(res[:], acc[piece, m][:])
                 nc.sync.dma_start(out[m * P : (m + 1) * P, v0:v1], res[:])
 
-        gather_first_centres(f"nb{(slot - 3) % 8}")
+        c_planes = [gather_centres(piece, f"nb{(slot - 8 + piece) % RING}") for piece in range(len(PIECES))]
+        c_grouped = [group_centres(0, c_planes[0])]
         words, scales = quantise(z_grouped[:].rearrange("p v u -> p (v u)").bitcast(BF16), V, "z")
         for piece, (v0, v1) in enumerate(PIECES):
             for m in range(2):
                 product(piece, m, 1, words[:, v0:v1], scales[:, v0:v1])
-        first = quantise_c(0)
-        ct = gather_last_centres(2, "z_grouped")
-        second = quantise_c(1, "h2")
-        cg = keep.tile([P, P, PACK], BF16, name="c_last", align_bytes=64)
-        nc.vector.tensor_copy(
-            cg[:].rearrange("p (c i) t -> p c t i", i=4), ct[:].rearrange("p t (c i) -> p c t i", i=4)
-        )
-        c_grouped.append(cg[:])
-        finish(0, *first)
-        finish(1, *second)
-        cw, cb = quantise_c(2)
-        finish(2, cw, cb)
+        c_grouped.append(group_centres(1, c_planes[1]))
+        finish(0, c_grouped[0])
+        c_grouped.append(group_centres(2, c_planes[2]))
+        finish(1, c_grouped[1])
+        finish(2, c_grouped[2])

@@ -1,7 +1,6 @@
 from contextlib import ExitStack
 
 import concourse.mybir as mybir
-from concourse.masks import make_identity
 
 K, T, S, V, H, N = 1024, 2048, 1024, 512, 512, 256
 FLOPS = 2 * K * H * S + 2 * 2 * H * N * V
@@ -23,10 +22,9 @@ K_PASS = P * PACK
 VEC, SCA = "vector", "scalar"
 PLANE_CUT = 384
 LAST_PLANE = ((VEC, 0, 256), (SCA, 256, 512), (SCA, 512, 768), (SCA, 768, 1024))
-H_BANKS = ((0, 1, 2, 3), (4, 5), (0, 1), (4, 5))
-SUM_BANKS = (2, 3, 6, 7)
-NEIGHBOURS = ((VEC, 0, 0, 4), (SCA, 2, 0, 4), (VEC, 1, 0, 4), (SCA, 3, 3, 4), (VEC, 3, 0, 3))
-RING = 10
+H_BANKS = ((0, 1, 2, 3), (4, 5), (6, 7), (0, 1))
+HALVES = ((0, 256), (256, 512))
+ADD = mybir.AluOpType.add
 PIECES = ((0, 256), (256, 384), (384, 512))
 OUT_BANKS = (4, 2, 6)
 
@@ -70,8 +68,6 @@ def tile_picked_sagecat_mean_e_kernel(
 
         w23_scales = keep.tile([P, 2 * N], U8, align_bytes=64)
         nc.vector.memset(w23_scales[:].bitcast(I32), 0)
-        ident = keep.tile([P, P], F32)
-        make_identity(nc, ident[:])
 
         offs_t = load_list(offs, "offs_t")
         x_raw = {}
@@ -202,67 +198,65 @@ def tile_picked_sagecat_mean_e_kernel(
         h_out(0, (1, 3))
         quantise_w(1, 2, 4)
         h_pass(1, 1)
-        h_out(1)
         for t in range(2, PACK):
             h_pass(t, 0)
             h_pass(t, 1)
-            h_out(t)
 
-        sums = [bank(b, [P, PACK, P], f"sums{vb}") for vb, b in enumerate(SUM_BANKS)]
-        zT = [keep.tile([P, 2, P, 2], BF16, name=f"zT{vb}", align_bytes=64) for vb in range(4)]
-        back = [bank(b, [P, 2, 2 * P], f"back{b}") for b in range(2)]
-        z_grouped = keep.tile([P, V, 2], F32, align_bytes=64)
-        slot = 0
-        for t in range(PACK):
-            added = [0] * 4
-            for engine, d, b0, b1 in NEIGHBOURS:
-                gt = work.tile([P, (b1 - b0) * P], F32, name=f"nb{t}_{d}_{b0}", tag=f"nb{slot % RING}", align_bytes=64)
-                slot = slot + 1
-                gather(engine, gt[:], h[t], pos_t[d][:, 8 * b0 : 8 * b1])
-                for vb in range(b0, b1):
-                    nc.tensor.matmul(
-                        out=sums[vb][:, t, :],
-                        lhsT=gt[:, (vb - b0) * P : (vb - b0 + 1) * P],
-                        rhs=ident[:],
-                        start=(added[vb] == 0),
-                        stop=(added[vb] == 3),
-                        is_transpose=True,
-                    )
-                    added[vb] = added[vb] + 1
-                    if t % 2 == 1 and added[vb] == 4:
-                        u = t // 2
-                        nc.scalar.activation(
-                            zT[vb][:, u],
-                            sums[vb][:, 2 * u : 2 * u + 2, :].rearrange("v e p -> v p e"),
-                            COPY,
-                            scale=0.25,
-                        )
-                        nc.tensor.transpose(
-                            back[vb // 2][:, u, (vb % 2) * P : (vb % 2 + 1) * P],
-                            zT[vb][:, u].rearrange("v p e -> v (p e)").bitcast(F32),
-                            ident[:],
-                        )
-                        if u == 1 and added[vb ^ 1] == 4:
-                            b = vb // 2
-                            nc.scalar.copy(z_grouped[:, b * 2 * P : (b + 1) * 2 * P, :], back[b][:].rearrange("p u v -> p v u"))
+        z_sum = keep.tile([P, PACK, V], F32, align_bytes=64)
+        c_planes = keep.tile([P, PACK, V], BF16, align_bytes=64)
+        gather(VEC, c_planes[:, 0, :], h[0], cen_t[:])
+        part = {}
 
-        def gather_centres(piece, tag):
+        def first_list(t):
+            for v0, v1 in HALVES:
+                first = work.tile([P, v1 - v0], F32, name=f"nb{t}_0_{v0}", tag=f"nb{t % 2}_0_{v0}", align_bytes=64)
+                gather(SCA, first[:], h[t], pos_t[0][:, v0 // 16 : v1 // 16])
+                part[t, v0] = first
+
+        def add_list(t, d, tags=(None, None)):
+            for (v0, v1), tag in zip(HALVES, tags):
+                nxt = work.tile([P, v1 - v0], F32, name=f"nb{t}_{d}_{v0}", tag=tag or f"nb{t % 2}_{d}_{v0}", align_bytes=64)
+                nc.vector.tensor_tensor(nxt[:], h[t][:].indirect(pos_t[d][:, v0 // 16 : v1 // 16]), part[t, v0][:], ADD)
+                part[t, v0] = nxt
+
+        def last_list(t, cuts):
+            for a, b in cuts:
+                v0 = a // 256 * 256
+                nc.vector.tensor_tensor(
+                    z_sum[:, t, a:b], h[t][:].indirect(pos_t[3][:, a // 16 : b // 16]), part[t, v0][:, a - v0 : b - v0], ADD
+                )
+
+        for t in range(PACK - 1):
+            first_list(t)
+            h_out(t + 1)
+            add_list(t, 1)
+            add_list(t, 2)
+            last_list(t, HALVES)
+        first_list(PACK - 1)
+        for t in range(1, PACK):
+            gather(SCA, c_planes[:, t, :], h[t], cen_t[:])
+        c_grouped = []
+        for v0, v1 in HALVES:
+            cg = work.tile([P, v1 - v0, PACK], BF16, name=f"c_grouped{v0}", tag=f"c_grouped{v0}", align_bytes=64)
+            interleave(SCA, cg[:], c_planes[:, :, v0:v1])
+            c_grouped.append(cg)
+
+        def group_z(engine, piece):
             v0, v1 = PIECES[piece]
-            ct = work.tile([P, PACK, v1 - v0], BF16, name=f"c_planes{piece}", tag=tag, align_bytes=64)
-            for t in range(PACK):
-                gather((VEC, SCA)[t % 2], ct[:, t, :], h[t], cen_t[:, v0 // 16 : v1 // 16])
-            return ct
-
-        def group_centres(piece, ct):
-            cg = keep.tile([P, ct.shape[2], PACK], BF16, name=f"c_grouped{piece}", align_bytes=64)
-            interleave(VEC, cg[:], ct[:])
-            return cg
+            zg = keep.tile([P, v1 - v0, PACK], BF16, name=f"z_grouped{piece}", align_bytes=64)
+            dst = zg[:].rearrange("p (c i) j -> p c j i", i=4)
+            src = z_sum[:, :, v0:v1].rearrange("p j (c i) -> p c j i", i=4)
+            if engine == VEC:
+                nc.vector.tensor_scalar_mul(dst, src, 0.25)
+            else:
+                nc.scalar.activation(dst, src, COPY, scale=0.25)
+            return zg
 
         acc = {}
 
         def product(piece, m, a, words, scales):
             v0, v1 = PIECES[piece]
-            if a == 1:
+            if a == 0:
                 acc[piece, m] = bank(OUT_BANKS[piece] + m, [P, v1 - v0], f"o_acc{piece}_{m}")
             nc.tensor.matmul_mx(
                 out=acc[piece, m][:],
@@ -270,30 +264,35 @@ def tile_picked_sagecat_mean_e_kernel(
                 lhsT_scale=w23_scales[:, a * N + m * P : a * N + (m + 1) * P],
                 rhs=words.bitcast(FP8X4),
                 rhs_scale=scales,
-                start=(a == 1),
-                stop=(a == 0),
+                start=(a == 0),
+                stop=(a == 1),
             )
 
         def finish(piece, cg):
             v0, v1 = PIECES[piece]
-            words, scales = quantise(cg[:].rearrange("p v t -> p (v t)"), v1 - v0, f"c{piece}")
+            words, scales = quantise(cg[:].rearrange("p v t -> p (v t)"), v1 - v0, f"z{piece}")
             for m in range(2):
-                product(piece, m, 0, words[:], scales[:])
+                product(piece, m, 1, words[:], scales[:])
                 res = keep.tile([P, v1 - v0], F32, name=f"res{piece}_{m}")
-                if (piece, m) == (2, 1):
+                if (piece, m) in ((0, 0), (1, 1)):
                     nc.vector.tensor_copy(res[:], acc[piece, m][:])
                 else:
                     nc.scalar.copy(res[:], acc[piece, m][:])
                 nc.sync.dma_start(out[m * P : (m + 1) * P, v0:v1], res[:])
 
-        c_planes = [gather_centres(piece, f"nb{(slot - 8 + piece) % RING}") for piece in range(len(PIECES))]
-        c_grouped = [group_centres(0, c_planes[0])]
-        words, scales = quantise(z_grouped[:].rearrange("p v u -> p (v u)").bitcast(BF16), V, "z")
-        for piece, (v0, v1) in enumerate(PIECES):
-            for m in range(2):
-                product(piece, m, 1, words[:, v0:v1], scales[:, v0:v1])
-        c_grouped.append(group_centres(1, c_planes[1]))
-        finish(0, c_grouped[0])
-        c_grouped.append(group_centres(2, c_planes[2]))
-        finish(1, c_grouped[1])
-        finish(2, c_grouped[2])
+        def centre_products(half, pieces):
+            v0, v1 = HALVES[half]
+            words, scales = quantise(c_grouped[half][:].rearrange("p v t -> p (v t)"), v1 - v0, f"c{half}")
+            for piece in pieces:
+                a, b = PIECES[piece]
+                for m in range(2):
+                    product(piece, m, 0, words[:, a - v0 : b - v0], scales[:, a - v0 : b - v0])
+
+        add_list(PACK - 1, 1)
+        centre_products(0, (0,))
+        add_list(PACK - 1, 2, (None, "c_grouped0"))
+        last_list(PACK - 1, PIECES)
+        centre_products(1, (1, 2))
+        z_grouped = [group_z(engine, piece) for piece, engine in enumerate((SCA, SCA, VEC))]
+        for piece in (0, 2, 1):
+            finish(piece, z_grouped[piece])

@@ -20,8 +20,10 @@ PACK = 4
 K_PASS = P * PACK
 
 VEC, SCA = "vector", "scalar"
-PLANE_CUT = 384
+PLANE_CUTS = ((384, 384, 384), (256, 256, 256))
+CLOSING_PLANE = ((VEC, 0, 256), (SCA, 256, 512), (SCA, 512, 1024))
 LAST_PLANE = ((VEC, 0, 256), (SCA, 256, 512), (SCA, 512, 768), (SCA, 768, 1024))
+W_CUT = 88
 H_BANKS = ((0, 1, 2, 3), (4, 5), (6, 7), (0, 1))
 HALVES = ((0, 256), (256, 512))
 ADD = mybir.AluOpType.add
@@ -101,15 +103,18 @@ def tile_picked_sagecat_mean_e_kernel(
         x_scales = {}
         x_grouped = {}
 
-        def gather_plane(g, j, cuts=((VEC, 0, PLANE_CUT), (SCA, PLANE_CUT, S))):
-            for engine, c0, c1 in cuts:
+        def gather_plane(g, j, cuts=None):
+            for engine, c0, c1 in cuts or ((VEC, 0, PLANE_CUTS[g][j]), (SCA, PLANE_CUTS[g][j], S)):
                 gather(engine, planes[g][:, j, c0:c1], x_raw[g, j], offs_t[:, c0 // 16 : c1 // 16])
 
-        def group_x(engine, g, c0, c1):
+        def group_x(g, u, c0, c1):
             half = c0 // 512
             if (g, half) not in x_grouped:
                 x_grouped[g, half] = keep.tile([P, 512, PACK], BF16, name=f"x_grouped{g}_{half}", align_bytes=64)
-            interleave(engine, x_grouped[g, half][:, c0 % 512 : c0 % 512 + c1 - c0, :], planes[g][:, :, c0:c1])
+            nc.vector.tensor_copy(
+                x_grouped[g, half][:, c0 % 512 : c0 % 512 + c1 - c0, 2 * u : 2 * u + 2],
+                planes[g][:, 2 * u : 2 * u + 2, c0:c1].rearrange("p j c -> p c j"),
+            )
 
         def quantise_x(g, c0, c1, tag=None):
             if g not in x_scales:
@@ -120,15 +125,20 @@ def tile_picked_sagecat_mean_e_kernel(
                 in_=x_grouped[g, c0 // 512][:, c0 % 512 : c0 % 512 + c1 - c0, :].rearrange("p c j -> p (c j)"),
             )
 
-        for j in range(PACK):
+        for j in range(3):
             gather_plane(0, j)
+        group_x(0, 0, 0, 512)
+        group_x(0, 0, 512, 1024)
+        gather_plane(0, 3, CLOSING_PLANE)
         gather_plane(1, 0)
-        group_x(VEC, 0, 0, 512)
-        gather_plane(1, 1)
+        group_x(0, 1, 0, 512)
+        group_x(0, 1, 512, 1024)
+        gather_plane(1, 1, CLOSING_PLANE)
         quantise_x(0, 0, 512)
-        group_x(VEC, 0, 512, 1024)
-        gather_plane(1, 2)
         quantise_x(0, 512, 1024)
+        gather_plane(1, 2)
+        group_x(1, 0, 0, 512)
+        group_x(1, 0, 512, 1024)
         gather_plane(1, 3, LAST_PLANE)
         w_grouped, w_words, w_scales = {}, {}, {}
 
@@ -142,9 +152,9 @@ def tile_picked_sagecat_mean_e_kernel(
             else:
                 nc.scalar.activation(dst, src, COPY)
 
-        def quantise_w(g, t0, t1):
+        def quantise_w(g, t0, t1, tag=None):
             src = w_grouped[g, t0 // 2][:, t0 % 2 : t0 % 2 + t1 - t0].rearrange("p t m j -> p (t m j)")
-            words, scales = quantise(src, (t1 - t0) * P, f"w{g}_{t0}")
+            words, scales = quantise(src, (t1 - t0) * P, f"w{g}_{t0}", tag)
             for t in range(t0, t1):
                 w_words[g, t] = words[:, (t - t0) * P : (t - t0 + 1) * P]
                 w_scales[g, t] = scales[:, (t - t0) * P : (t - t0 + 1) * P]
@@ -178,23 +188,25 @@ def tile_picked_sagecat_mean_e_kernel(
                     nc.scalar.activation(dst, h_acc[t][part][:], RELU)
             h[t] = ht
 
-        cast_w(SCA, 0, 0)
+        group_x(1, 1, 256, 512)
+        group_x(1, 1, 0, 256)
+        group_x(1, 1, 512, 768)
+        group_x(1, 1, 768, 1024)
+        cast_w(SCA, 0, 0, 0, W_CUT)
+        cast_w(VEC, 0, 0, W_CUT, P)
         cast_w(SCA, 0, 1)
         quantise_w(0, 0, 2)
-        group_x(VEC, 1, 256, 512)
-        group_x(VEC, 1, 0, 256)
-        group_x(VEC, 1, 512, 768)
-        group_x(VEC, 1, 768, 1024)
         quantise_x(1, 0, 512, tag="w_grouped0_0")
         quantise_x(1, 512, 1024)
         h_pass(0, 0)
         h_pass(1, 0)
-        cast_w(SCA, 1, 0)
+        cast_w(SCA, 1, 0, 0, W_CUT)
+        cast_w(VEC, 1, 0, W_CUT, P)
         quantise_w(1, 0, 1)
         cast_w(SCA, 1, 1)
         quantise_w(1, 1, 2)
-        quantise_w(0, 2, 4)
         h_pass(0, 1)
+        quantise_w(0, 2, 4, tag="w_grouped1_0")
         h_out(0, (1, 3))
         quantise_w(1, 2, 4)
         h_pass(1, 1)

@@ -27,6 +27,8 @@ W_CUT = 88
 H_BANKS = ((0, 1, 2, 3), (4, 5), (6, 7), (0, 1))
 HALVES = ((0, 256), (256, 512))
 ADD = mybir.AluOpType.add
+MAX = mybir.AluOpType.max
+MULT = mybir.AluOpType.mult
 PIECES = ((0, 256), (256, 384), (384, 512))
 OUT_BANKS = (4, 2, 6)
 
@@ -54,13 +56,6 @@ def tile_picked_sagecat_mean_e_kernel(
                 nc.vector.tensor_copy(dst, window[:].indirect(offsets))
             else:
                 nc.scalar.activation(dst, window[:].indirect(offsets), COPY)
-
-        def interleave(engine, dst, src):
-            views = (dst.rearrange("p (c i) j -> p c j i", i=4), src.rearrange("p j (c i) -> p c j i", i=4))
-            if engine == VEC:
-                nc.vector.tensor_copy(*views)
-            else:
-                nc.scalar.copy(*views)
 
         def quantise(src, n, name, tag=None):
             words = keep.tile([P, n], U32, name=f"{name}_words", align_bytes=64)
@@ -183,9 +178,9 @@ def tile_picked_sagecat_mean_e_kernel(
             for part in range(len(H_BANKS[t])):
                 dst = ht[:, part * width : (part + 1) * width]
                 if part in on_vector:
-                    nc.vector.tensor_scalar_max(dst, h_acc[t][part][:], 0.0)
+                    nc.vector.tensor_scalar(dst, h_acc[t][part][:], 0.0, 0.25, MAX, MULT)
                 else:
-                    nc.scalar.activation(dst, h_acc[t][part][:], RELU)
+                    nc.scalar.activation(dst, h_acc[t][part][:], RELU, scale=0.25)
             h[t] = ht
 
         group_x(1, 1, 256, 512)
@@ -214,61 +209,50 @@ def tile_picked_sagecat_mean_e_kernel(
             h_pass(t, 0)
             h_pass(t, 1)
 
-        z_sum = keep.tile([P, PACK, V], F32, align_bytes=64)
-        c_planes = keep.tile([P, PACK, V], BF16, align_bytes=64)
-        gather(VEC, c_planes[:, 0, :], h[0], cen_t[:])
-        part = {}
+        pair_sums = [keep.tile([P, PACK, V], F32, name=f"pair_sums{r}", align_bytes=64) for r in range(2)]
+        for t in range(PACK):
+            first = []
+            for r in range(2):
+                ft = work.tile([P, V], F32, name=f"nb{t}_{r}", tag=f"nb{t}_{r}", align_bytes=64)
+                gather(VEC if (t, r) == (0, 1) else SCA, ft[:], h[t], pos_t[2 * r][:])
+                first.append(ft)
+            for r in range(2):
+                nc.vector.tensor_tensor(pair_sums[r][:, t, :], h[t][:].indirect(pos_t[2 * r + 1][:]), first[r][:], ADD)
+            if t + 1 < PACK:
+                h_out(t + 1, () if t == 1 else (1,))
+        z_grouped = keep.tile([P, V, PACK], BF16, align_bytes=64)
 
-        def first_list(t):
-            for v0, v1 in HALVES:
-                first = work.tile([P, v1 - v0], F32, name=f"nb{t}_0_{v0}", tag=f"nb{t % 2}_0_{v0}", align_bytes=64)
-                gather(SCA, first[:], h[t], pos_t[0][:, v0 // 16 : v1 // 16])
-                part[t, v0] = first
+        def group_z(v0, v1):
+            nc.vector.tensor_tensor(
+                z_grouped[:, v0:v1, :].rearrange("p (c i) j -> p c j i", i=4),
+                pair_sums[0][:, :, v0:v1].rearrange("p j (c i) -> p c j i", i=4),
+                pair_sums[1][:, :, v0:v1].rearrange("p j (c i) -> p c j i", i=4),
+                ADD,
+            )
 
-        def add_list(t, d, tags=(None, None)):
-            for (v0, v1), tag in zip(HALVES, tags):
-                nxt = work.tile([P, v1 - v0], F32, name=f"nb{t}_{d}_{v0}", tag=tag or f"nb{t % 2}_{d}_{v0}", align_bytes=64)
-                nc.vector.tensor_tensor(nxt[:], h[t][:].indirect(pos_t[d][:, v0 // 16 : v1 // 16]), part[t, v0][:], ADD)
-                part[t, v0] = nxt
-
-        def last_list(t, cuts):
-            for a, b in cuts:
-                v0 = a // 256 * 256
-                nc.vector.tensor_tensor(
-                    z_sum[:, t, a:b], h[t][:].indirect(pos_t[3][:, a // 16 : b // 16]), part[t, v0][:, a - v0 : b - v0], ADD
-                )
-
-        for t in range(PACK - 1):
-            first_list(t)
-            h_out(t + 1)
-            add_list(t, 1)
-            add_list(t, 2)
-            last_list(t, HALVES)
-        first_list(PACK - 1)
-        for t in range(1, PACK):
-            gather(SCA, c_planes[:, t, :], h[t], cen_t[:])
-        c_grouped = []
-        for v0, v1 in HALVES:
-            cg = work.tile([P, v1 - v0, PACK], BF16, name=f"c_grouped{v0}", tag=f"c_grouped{v0}", align_bytes=64)
-            interleave(SCA, cg[:], c_planes[:, :, v0:v1])
-            c_grouped.append(cg)
-
-        def group_z(engine, piece):
+        def gather_centres(piece, tag):
             v0, v1 = PIECES[piece]
-            zg = keep.tile([P, v1 - v0, PACK], BF16, name=f"z_grouped{piece}", align_bytes=64)
-            dst = zg[:].rearrange("p (c i) j -> p c j i", i=4)
-            src = z_sum[:, :, v0:v1].rearrange("p j (c i) -> p c j i", i=4)
+            ct = work.tile([P, PACK, v1 - v0], BF16, name=f"c_planes{piece}", tag=tag, align_bytes=64)
+            for t in range(PACK):
+                gather(SCA, ct[:, t, :], h[t], cen_t[:, v0 // 16 : v1 // 16])
+            return ct
+
+        def group_centres(engine, piece):
+            ct = c_planes[piece]
+            cg = keep.tile([P, ct.shape[2], PACK], BF16, name=f"c_grouped{piece}", align_bytes=64)
+            dst = cg[:].rearrange("p (c i) j -> p c j i", i=4)
+            src = ct[:].rearrange("p j (c i) -> p c j i", i=4)
             if engine == VEC:
-                nc.vector.tensor_scalar_mul(dst, src, 0.25)
+                nc.vector.tensor_scalar_mul(dst, src, 4.0)
             else:
-                nc.scalar.activation(dst, src, COPY, scale=0.25)
-            return zg
+                nc.scalar.activation(dst, src, COPY, scale=4.0)
+            return cg
 
         acc = {}
 
         def product(piece, m, a, words, scales):
             v0, v1 = PIECES[piece]
-            if a == 0:
+            if a == 1:
                 acc[piece, m] = bank(OUT_BANKS[piece] + m, [P, v1 - v0], f"o_acc{piece}_{m}")
             nc.tensor.matmul_mx(
                 out=acc[piece, m][:],
@@ -276,35 +260,44 @@ def tile_picked_sagecat_mean_e_kernel(
                 lhsT_scale=w23_scales[:, a * N + m * P : a * N + (m + 1) * P],
                 rhs=words.bitcast(FP8X4),
                 rhs_scale=scales,
-                start=(a == 0),
-                stop=(a == 1),
+                start=(a == 1),
+                stop=(a == 0),
             )
 
-        def finish(piece, cg):
+        def z_products(v0, v1):
+            words, scales = quantise(z_grouped[:, v0:v1, :].rearrange("p v t -> p (v t)"), v1 - v0, f"z{v0}")
+            for piece, (a, b) in enumerate(PIECES):
+                if v0 <= a < v1:
+                    for m in range(2):
+                        product(piece, m, 1, words[:, a - v0 : b - v0], scales[:, a - v0 : b - v0])
+
+        def centre_products(piece, cg):
             v0, v1 = PIECES[piece]
-            words, scales = quantise(cg[:].rearrange("p v t -> p (v t)"), v1 - v0, f"z{piece}")
+            words, scales = quantise(cg[:].rearrange("p v t -> p (v t)"), v1 - v0, f"c{piece}")
             for m in range(2):
-                product(piece, m, 1, words[:], scales[:])
+                product(piece, m, 0, words[:], scales[:])
+
+        def store(piece, on_vector=()):
+            v0, v1 = PIECES[piece]
+            for m in range(2):
                 res = keep.tile([P, v1 - v0], F32, name=f"res{piece}_{m}")
-                if (piece, m) in ((0, 0), (1, 1)):
+                if m in on_vector:
                     nc.vector.tensor_copy(res[:], acc[piece, m][:])
                 else:
                     nc.scalar.copy(res[:], acc[piece, m][:])
                 nc.sync.dma_start(out[m * P : (m + 1) * P, v0:v1], res[:])
 
-        def centre_products(half, pieces):
-            v0, v1 = HALVES[half]
-            words, scales = quantise(c_grouped[half][:].rearrange("p v t -> p (v t)"), v1 - v0, f"c{half}")
-            for piece in pieces:
-                a, b = PIECES[piece]
-                for m in range(2):
-                    product(piece, m, 0, words[:, a - v0 : b - v0], scales[:, a - v0 : b - v0])
-
-        add_list(PACK - 1, 1)
-        centre_products(0, (0,))
-        add_list(PACK - 1, 2, (None, "c_grouped0"))
-        last_list(PACK - 1, PIECES)
-        centre_products(1, (1, 2))
-        z_grouped = [group_z(engine, piece) for piece, engine in enumerate((SCA, SCA, VEC))]
-        for piece in (0, 2, 1):
-            finish(piece, z_grouped[piece])
+        c_planes = [gather_centres(piece, tag) for piece, tag in enumerate(("nb2_0", "nb2_1", "nb3_0"))]
+        group_z(*HALVES[0])
+        c_grouped0 = group_centres(VEC, 0)
+        z_products(*HALVES[0])
+        centre_products(0, c_grouped0)
+        group_z(*HALVES[1])
+        c_grouped2 = group_centres(SCA, 2)
+        store(0)
+        c_grouped1 = group_centres(VEC, 1)
+        z_products(*HALVES[1])
+        centre_products(1, c_grouped1)
+        centre_products(2, c_grouped2)
+        store(1, (1,))
+        store(2, (1,))

@@ -23,7 +23,7 @@ VEC, SCA = "vector", "scalar"
 PLANE_CUTS = ((384, 384, 384), (256, 256, 256))
 CLOSING_PLANE = ((VEC, 0, 256), (SCA, 256, 512), (SCA, 512, 1024))
 LAST_PLANE = ((VEC, 0, 256), (SCA, 256, 512), (SCA, 512, 768), (SCA, 768, 1024))
-W_CUT = 88
+W_CUT = 48
 H_BANKS = ((0, 1, 2, 3), (4, 5), (6, 7), (0, 1))
 HALVES = ((0, 256), (256, 512))
 ADD = mybir.AluOpType.add
@@ -66,7 +66,6 @@ def tile_picked_sagecat_mean_e_kernel(
         w23_scales = keep.tile([P, 2 * N], U8, align_bytes=64)
         nc.vector.memset(w23_scales[:].bitcast(I32), 0)
 
-        offs_t = load_list(offs, "offs_t")
         x_raw = {}
         for g in range(passes):
             rows = xT[g * K_PASS : (g + 1) * K_PASS, :].rearrange("(p j) c -> p j c", j=PACK)
@@ -74,6 +73,8 @@ def tile_picked_sagecat_mean_e_kernel(
                 raw = keep.tile([P, T], F32, name=f"x_raw_{g}_{j}")
                 nc.sync.dma_start(raw[:], rows[:, j, :])
                 x_raw[g, j] = raw
+                if (g, j) == (0, 0):
+                    offs_t = load_list(offs, "offs_t")
         w_raw = []
         for g in range(passes):
             raw = keep.tile([P, PACK, H], F32, name=f"w_raw_{g}")
@@ -111,6 +112,13 @@ def tile_picked_sagecat_mean_e_kernel(
                 planes[g][:, 2 * u : 2 * u + 2, c0:c1].rearrange("p j c -> p c j"),
             )
 
+        def group_whole(g, half):
+            x_grouped[g, half] = keep.tile([P, 512, PACK], BF16, name=f"x_grouped{g}_{half}", align_bytes=64)
+            nc.vector.tensor_copy(
+                x_grouped[g, half][:].rearrange("p (c i) j -> p c j i", i=4),
+                planes[g][:, :, 512 * half : 512 * half + 512].rearrange("p j (c i) -> p c j i", i=4),
+            )
+
         def quantise_x(g, c0, c1, tag=None):
             if g not in x_scales:
                 x_scales[g] = work.tile([P, S], U8, name=f"x_scales{g}", tag=tag or f"x_scales{g}", align_bytes=64)
@@ -121,18 +129,16 @@ def tile_picked_sagecat_mean_e_kernel(
             )
 
         for j in range(3):
-            gather_plane(0, j)
-        group_x(0, 0, 0, 512)
-        group_x(0, 0, 512, 1024)
-        gather_plane(0, 3, CLOSING_PLANE)
-        gather_plane(1, 0)
-        group_x(0, 1, 0, 512)
-        group_x(0, 1, 512, 1024)
-        gather_plane(1, 1, CLOSING_PLANE)
+            gather_plane(0, j, ((VEC, 0, 512), (SCA, 512, S)))
+        gather_plane(0, 3, ((VEC, 0, 512), (SCA, 512, S)))
+        group_whole(0, 0)
+        group_whole(0, 1)
+        gather_plane(1, 0, ((SCA, 0, S),))
         quantise_x(0, 0, 512)
         quantise_x(0, 512, 1024)
-        gather_plane(1, 2)
+        gather_plane(1, 1, CLOSING_PLANE)
         group_x(1, 0, 0, 512)
+        gather_plane(1, 2, ((VEC, 0, 384), (SCA, 384, S)))
         group_x(1, 0, 512, 1024)
         gather_plane(1, 3, LAST_PLANE)
         w_grouped, w_words, w_scales = {}, {}, {}
@@ -186,24 +192,37 @@ def tile_picked_sagecat_mean_e_kernel(
         group_x(1, 1, 256, 512)
         group_x(1, 1, 0, 256)
         group_x(1, 1, 512, 768)
+        quantise_x(1, 0, 512)
+        for half in range(2):
+            warm = bank(6 + half, [P, 512], f"warm{half}")
+            nc.tensor.matmul_mx(
+                out=warm[:],
+                lhsT=x_words[1][:, 0:128].bitcast(FP8X4),
+                lhsT_scale=x_scales[1][:, 0:128],
+                rhs=x_words[0][:, 0:512].bitcast(FP8X4),
+                rhs_scale=x_scales[0][:, 0:512],
+                start=True,
+                stop=True,
+            )
         group_x(1, 1, 768, 1024)
-        cast_w(SCA, 0, 0, 0, W_CUT)
-        cast_w(VEC, 0, 0, W_CUT, P)
+        quantise_x(1, 512, 768)
+        quantise_x(1, 768, 1024)
+        cast_w(SCA, 0, 0)
         cast_w(SCA, 0, 1)
-        quantise_w(0, 0, 2)
-        quantise_x(1, 0, 512, tag="w_grouped0_0")
-        quantise_x(1, 512, 1024)
+        quantise_w(0, 0, 1)
         h_pass(0, 0)
-        h_pass(1, 0)
         cast_w(SCA, 1, 0, 0, W_CUT)
         cast_w(VEC, 1, 0, W_CUT, P)
         quantise_w(1, 0, 1)
-        cast_w(SCA, 1, 1)
+        cast_w(SCA, 1, 1, 0, 72)
         quantise_w(1, 1, 2)
+        cast_w(VEC, 1, 1, 72, P)
         h_pass(0, 1)
-        quantise_w(0, 2, 4, tag="w_grouped1_0")
-        h_out(0, (1, 3))
+        quantise_w(0, 1, 2, tag="w_grouped1_0")
+        h_out(0, (3,))
+        quantise_w(0, 2, 4, tag="w_grouped0_0")
         quantise_w(1, 2, 4)
+        h_pass(1, 0)
         h_pass(1, 1)
         for t in range(2, PACK):
             h_pass(t, 0)
@@ -216,10 +235,10 @@ def tile_picked_sagecat_mean_e_kernel(
                 ft = work.tile([P, V], F32, name=f"nb{t}_{r}", tag=f"nb{t}_{r}", align_bytes=64)
                 gather(VEC if (t, r) == (0, 1) else SCA, ft[:], h[t], pos_t[2 * r][:])
                 first.append(ft)
-            for r in range(2):
-                nc.vector.tensor_tensor(pair_sums[r][:, t, :], h[t][:].indirect(pos_t[2 * r + 1][:]), first[r][:], ADD)
             if t + 1 < PACK:
                 h_out(t + 1, () if t == 1 else (1,))
+            for r in range(2):
+                nc.vector.tensor_tensor(pair_sums[r][:, t, :], h[t][:].indirect(pos_t[2 * r + 1][:]), first[r][:], ADD)
         z_grouped = keep.tile([P, V, PACK], BF16, align_bytes=64)
 
         def group_z(v0, v1):
@@ -230,18 +249,20 @@ def tile_picked_sagecat_mean_e_kernel(
                 ADD,
             )
 
-        def gather_centres(piece, tag):
-            v0, v1 = PIECES[piece]
-            ct = work.tile([P, PACK, v1 - v0], BF16, name=f"c_planes{piece}", tag=tag, align_bytes=64)
+        def gather_centres(half, tag, last_cuts):
+            v0, v1 = HALVES[half]
+            ct = work.tile([P, PACK, v1 - v0], BF16, name=f"c_planes{half}", tag=tag, align_bytes=64)
             for t in range(PACK):
-                gather(SCA, ct[:, t, :], h[t], cen_t[:, v0 // 16 : v1 // 16])
+                for a, b in last_cuts if t == PACK - 1 else ((v0, v1),):
+                    gather(SCA, ct[:, t, a - v0 : b - v0], h[t], cen_t[:, a // 16 : b // 16])
             return ct
 
         def group_centres(engine, piece):
-            ct = c_planes[piece]
-            cg = keep.tile([P, ct.shape[2], PACK], BF16, name=f"c_grouped{piece}", align_bytes=64)
+            v0, v1 = PIECES[piece]
+            ct = c_planes[v0 // 256][:, :, v0 % 256 : v0 % 256 + v1 - v0]
+            cg = keep.tile([P, v1 - v0, PACK], BF16, name=f"c_grouped{piece}", align_bytes=64)
             dst = cg[:].rearrange("p (c i) j -> p c j i", i=4)
-            src = ct[:].rearrange("p j (c i) -> p c j i", i=4)
+            src = ct.rearrange("p j (c i) -> p c j i", i=4)
             if engine == VEC:
                 nc.vector.tensor_scalar_mul(dst, src, 4.0)
             else:
@@ -287,7 +308,7 @@ def tile_picked_sagecat_mean_e_kernel(
                     nc.scalar.copy(res[:], acc[piece, m][:])
                 nc.sync.dma_start(out[m * P : (m + 1) * P, v0:v1], res[:])
 
-        c_planes = [gather_centres(piece, tag) for piece, tag in enumerate(("nb2_0", "nb2_1", "nb3_0"))]
+        c_planes = [gather_centres(0, "nb2_0", PIECES[:1]), gather_centres(1, "nb2_1", PIECES[1:])]
         group_z(*HALVES[0])
         c_grouped0 = group_centres(VEC, 0)
         z_products(*HALVES[0])

@@ -193,17 +193,6 @@ def tile_picked_sagecat_mean_e_kernel(
         group_x(1, 1, 0, 256)
         group_x(1, 1, 512, 768)
         quantise_x(1, 0, 512)
-        for half in range(2):
-            warm = bank(6 + half, [P, 512], f"warm{half}")
-            nc.tensor.matmul_mx(
-                out=warm[:],
-                lhsT=x_words[1][:, 0:128].bitcast(FP8X4),
-                lhsT_scale=x_scales[1][:, 0:128],
-                rhs=x_words[0][:, 0:512].bitcast(FP8X4),
-                rhs_scale=x_scales[0][:, 0:512],
-                start=True,
-                stop=True,
-            )
         group_x(1, 1, 768, 1024)
         quantise_x(1, 512, 768)
         quantise_x(1, 768, 1024)

from contextlib import ExitStack

import concourse.mybir as mybir

K, T, S, V, H, N = 1024, 2048, 1024, 512, 512, 256
FLOPS = 2 * K * H * S + 2 * 2 * H * N * V

F32 = mybir.dt.float32
BF16 = mybir.dt.bfloat16
I32 = mybir.dt.int32
U32 = mybir.dt.uint32
U16 = mybir.dt.uint16
U8 = mybir.dt.uint8
FP8X4 = mybir.dt.float8_e4m3fn_x4
COPY = mybir.ActivationFunctionType.Copy
RELU = mybir.ActivationFunctionType.Relu

P = 128
PACK = 4
K_PASS = P * PACK

VEC, SCA = "vector", "scalar"
PLANE_CUTS = ((384, 384, 384), (256, 256, 256))
CLOSING_PLANE = ((VEC, 0, 256), (SCA, 256, 512), (SCA, 512, 1024))
LAST_PLANE = ((VEC, 0, 256), (SCA, 256, 512), (SCA, 512, 768), (SCA, 768, 1024))
W_CUT = 48
H_BANKS = ((0, 1, 2, 3), (4, 5), (6, 7), (0, 1))
HALVES = ((0, 256), (256, 512))
ADD = mybir.AluOpType.add
MAX = mybir.AluOpType.max
MULT = mybir.AluOpType.mult
PIECES = ((0, 256), (256, 384), (384, 512))
OUT_BANKS = (4, 2, 6)


def tile_picked_sagecat_mean_e_kernel(
    tc, xT, w1, w2_words, w2_scales, w3_words, w3_scales, offs, cen, pos1, pos2, pos3, pos4, out
):
    nc = tc.nc
    passes = K // K_PASS
    with ExitStack() as ctx:
        keep = ctx.enter_context(tc.tile_pool(name="keep", bufs=1))
        work = ctx.enter_context(tc.tile_pool(name="work", bufs=1))
        psum = ctx.enter_context(tc.psum_pool(name="psum", bufs=1))

        def bank(b, shape, name):
            return psum.tile(shape, F32, name=name, tag=f"bank{b}")

        def load_list(src, name):
            t = keep.tile(list(src.shape), U16, name=name)
            nc.sync.dma_start(t[:], src)
            return t

        def gather(engine, dst, window, offsets):
            if engine == VEC:
                nc.vector.tensor_copy(dst, window[:].indirect(offsets))
            else:
                nc.scalar.activation(dst, window[:].indirect(offsets), COPY)

        def quantise(src, n, name, tag=None):
            words = keep.tile([P, n], U32, name=f"{name}_words", align_bytes=64)
            scales = work.tile([P, n], U8, name=f"{name}_scales", tag=tag or f"{name}_scales", align_bytes=64)
            nc.vector.quantize_mx(out=words[:].bitcast(FP8X4), scales=scales[:], in_=src)
            return words, scales

        w23_scales = keep.tile([P, 2 * N], U8, align_bytes=64)
        nc.vector.memset(w23_scales[:].bitcast(I32), 0)

        x_raw = {}
        for g in range(passes):
            rows = xT[g * K_PASS : (g + 1) * K_PASS, :].rearrange("(p j) c -> p j c", j=PACK)
            for j in range(PACK):
                raw = keep.tile([P, T], F32, name=f"x_raw_{g}_{j}")
                nc.sync.dma_start(raw[:], rows[:, j, :])
                x_raw[g, j] = raw
                if (g, j) == (0, 0):
                    offs_t = load_list(offs, "offs_t")
        w_raw = []
        for g in range(passes):
            raw = keep.tile([P, PACK, H], F32, name=f"w_raw_{g}")
            nc.sync.dma_start(raw[:], w1[g * K_PASS : (g + 1) * K_PASS, :].rearrange("(p j) c -> p j c", j=PACK))
            w_raw.append(raw)
        pos_t = [load_list(src, f"pos_t{d}") for d, src in enumerate((pos1, pos2, pos3, pos4))]
        cen_t = load_list(cen, "cen_t")
        w23_words = []
        for a, words in enumerate((w2_words, w3_words)):
            wt = keep.tile([P, N], I32, name=f"w23_words{a}", align_bytes=64)
            nc.sync.dma_start(wt[:], words[0].rearrange("p n t -> p (n t)").bitcast(I32))
            w23_words.append(wt)
        for a, scales in enumerate((w2_scales, w3_scales)):
            for q in range(4):
                nc.sync.dma_start(
                    w23_scales[32 * q : 32 * q + 4, a * N : (a + 1) * N].bitcast(I32),
                    scales[0, 4 * q : 4 * q + 4, :].bitcast(I32),
                )

        planes = [keep.tile([P, PACK, S], BF16, name=f"planes{g}", align_bytes=64) for g in range(passes)]
        x_words = [keep.tile([P, S], U32, name=f"x_words{g}", align_bytes=64) for g in range(passes)]
        x_scales = {}
        x_grouped = {}

        def gather_plane(g, j, cuts=None):
            for engine, c0, c1 in cuts or ((VEC, 0, PLANE_CUTS[g][j]), (SCA, PLANE_CUTS[g][j], S)):
                gather(engine, planes[g][:, j, c0:c1], x_raw[g, j], offs_t[:, c0 // 16 : c1 // 16])

        def group_x(g, u, c0, c1):
            half = c0 // 512
            if (g, half) not in x_grouped:
                x_grouped[g, half] = keep.tile([P, 512, PACK], BF16, name=f"x_grouped{g}_{half}", align_bytes=64)
            nc.vector.tensor_copy(
                x_grouped[g, half][:, c0 % 512 : c0 % 512 + c1 - c0, 2 * u : 2 * u + 2],
                planes[g][:, 2 * u : 2 * u + 2, c0:c1].rearrange("p j c -> p c j"),
            )

        def group_whole(g, half):
            x_grouped[g, half] = keep.tile([P, 512, PACK], BF16, name=f"x_grouped{g}_{half}", align_bytes=64)
            nc.vector.tensor_copy(
                x_grouped[g, half][:].rearrange("p (c i) j -> p c j i", i=4),
                planes[g][:, :, 512 * half : 512 * half + 512].rearrange("p j (c i) -> p c j i", i=4),
            )

        def quantise_x(g, c0, c1, tag=None):
            if g not in x_scales:
                x_scales[g] = work.tile([P, S], U8, name=f"x_scales{g}", tag=tag or f"x_scales{g}", align_bytes=64)
            nc.vector.quantize_mx(
                out=x_words[g][:, c0:c1].bitcast(FP8X4),
                scales=x_scales[g][:, c0:c1],
                in_=x_grouped[g, c0 // 512][:, c0 % 512 : c0 % 512 + c1 - c0, :].rearrange("p c j -> p (c j)"),
            )

        for j in range(3):
            gather_plane(0, j, ((VEC, 0, 512), (SCA, 512, S)))
        gather_plane(0, 3, ((VEC, 0, 512), (SCA, 512, S)))
        group_whole(0, 0)
        group_whole(0, 1)
        gather_plane(1, 0, ((SCA, 0, S),))
        quantise_x(0, 0, 512)
        quantise_x(0, 512, 1024)
        gather_plane(1, 1, CLOSING_PLANE)
        group_x(1, 0, 0, 512)
        gather_plane(1, 2, ((VEC, 0, 384), (SCA, 384, S)))
        group_x(1, 0, 512, 1024)
        gather_plane(1, 3, LAST_PLANE)
        w_grouped, w_words, w_scales = {}, {}, {}

        def cast_w(engine, g, u, m0=0, m1=P):
            if (g, u) not in w_grouped:
                w_grouped[g, u] = work.tile([P, 2, P, PACK], BF16, name=f"w_grouped{g}_{u}", tag=f"w_grouped{g}_{u}", align_bytes=64)
            src = w_raw[g][:].rearrange("p j (m t) -> p m j t", t=PACK)[:, m0:m1, :, 2 * u : 2 * u + 2]
            dst = w_grouped[g, u][:, :, m0:m1, :].rearrange("p t m j -> p m j t")
            if engine == VEC:
                nc.vector.tensor_copy(dst, src)
            else:
                nc.scalar.activation(dst, src, COPY)

        def quantise_w(g, t0, t1, tag=None):
            src = w_grouped[g, t0 // 2][:, t0 % 2 : t0 % 2 + t1 - t0].rearrange("p t m j -> p (t m j)")
            words, scales = quantise(src, (t1 - t0) * P, f"w{g}_{t0}", tag)
            for t in range(t0, t1):
                w_words[g, t] = words[:, (t - t0) * P : (t - t0 + 1) * P]
                w_scales[g, t] = scales[:, (t - t0) * P : (t - t0 + 1) * P]

        h, h_acc = {}, {}

        def h_pass(t, g):
            width = S // len(H_BANKS[t])
            if g == 0:
                h_acc[t] = [bank(b, [P, width], f"h_acc{t}_{b}") for b in H_BANKS[t]]
            for part in range(len(H_BANKS[t])):
                cols = slice(part * width, (part + 1) * width)
                nc.tensor.matmul_mx(
                    out=h_acc[t][part][:],
                    lhsT=w_words[g, t].bitcast(FP8X4),
                    lhsT_scale=w_scales[g, t],
                    rhs=x_words[g][:, cols].bitcast(FP8X4),
                    rhs_scale=x_scales[g][:, cols],
                    start=(g == 0),
                    stop=(g == passes - 1),
                )

        def h_out(t, on_vector=()):
            ht = keep.tile([P, S], F32, name=f"h{t}", align_bytes=64)
            width = S // len(H_BANKS[t])
            for part in range(len(H_BANKS[t])):
                dst = ht[:, part * width : (part + 1) * width]
                if part in on_vector:
                    nc.vector.tensor_scalar(dst, h_acc[t][part][:], 0.0, 0.25, MAX, MULT)
                else:
                    nc.scalar.activation(dst, h_acc[t][part][:], RELU, scale=0.25)
            h[t] = ht

        group_x(1, 1, 256, 512)
        group_x(1, 1, 0, 256)
        group_x(1, 1, 512, 768)
        quantise_x(1, 0, 512)
        group_x(1, 1, 768, 1024)
        quantise_x(1, 512, 768)
        quantise_x(1, 768, 1024)
        cast_w(SCA, 0, 0)
        cast_w(SCA, 0, 1)
        quantise_w(0, 0, 1)
        h_pass(0, 0)
        cast_w(SCA, 1, 0, 0, W_CUT)
        cast_w(VEC, 1, 0, W_CUT, P)
        quantise_w(1, 0, 1)
        cast_w(SCA, 1, 1, 0, 72)
        quantise_w(1, 1, 2)
        cast_w(VEC, 1, 1, 72, P)
        h_pass(0, 1)
        quantise_w(0, 1, 2, tag="w_grouped1_0")
        h_out(0, (3,))
        quantise_w(0, 2, 4, tag="w_grouped0_0")
        quantise_w(1, 2, 4)
        h_pass(1, 0)
        h_pass(1, 1)
        for t in range(2, PACK):
            h_pass(t, 0)
            h_pass(t, 1)

        pair_sums = [keep.tile([P, PACK, V], F32, name=f"pair_sums{r}", align_bytes=64) for r in range(2)]
        for t in range(PACK):
            first = []
            for r in range(2):
                ft = work.tile([P, V], F32, name=f"nb{t}_{r}", tag=f"nb{t}_{r}", align_bytes=64)
                gather(VEC if (t, r) == (0, 1) else SCA, ft[:], h[t], pos_t[2 * r][:])
                first.append(ft)
            if t + 1 < PACK:
                h_out(t + 1, () if t == 1 else (1,))
            for r in range(2):
                nc.vector.tensor_tensor(pair_sums[r][:, t, :], h[t][:].indirect(pos_t[2 * r + 1][:]), first[r][:], ADD)
        z_grouped = keep.tile([P, V, PACK], BF16, align_bytes=64)

        def group_z(v0, v1):
            nc.vector.tensor_tensor(
                z_grouped[:, v0:v1, :].rearrange("p (c i) j -> p c j i", i=4),
                pair_sums[0][:, :, v0:v1].rearrange("p j (c i) -> p c j i", i=4),
                pair_sums[1][:, :, v0:v1].rearrange("p j (c i) -> p c j i", i=4),
                ADD,
            )

        def gather_centres(half, tag, last_cuts):
            v0, v1 = HALVES[half]
            ct = work.tile([P, PACK, v1 - v0], BF16, name=f"c_planes{half}", tag=tag, align_bytes=64)
            for t in range(PACK):
                for a, b in last_cuts if t == PACK - 1 else ((v0, v1),):
                    gather(SCA, ct[:, t, a - v0 : b - v0], h[t], cen_t[:, a // 16 : b // 16])
            return ct

        def group_centres(engine, piece):
            v0, v1 = PIECES[piece]
            ct = c_planes[v0 // 256][:, :, v0 % 256 : v0 % 256 + v1 - v0]
            cg = keep.tile([P, v1 - v0, PACK], BF16, name=f"c_grouped{piece}", align_bytes=64)
            dst = cg[:].rearrange("p (c i) j -> p c j i", i=4)
            src = ct.rearrange("p j (c i) -> p c j i", i=4)
            if engine == VEC:
                nc.vector.tensor_scalar_mul(dst, src, 4.0)
            else:
                nc.scalar.activation(dst, src, COPY, scale=4.0)
            return cg

        acc = {}

        def product(piece, m, a, words, scales):
            v0, v1 = PIECES[piece]
            if a == 1:
                acc[piece, m] = bank(OUT_BANKS[piece] + m, [P, v1 - v0], f"o_acc{piece}_{m}")
            nc.tensor.matmul_mx(
                out=acc[piece, m][:],
                lhsT=w23_words[a][:, m * P : (m + 1) * P].bitcast(FP8X4),
                lhsT_scale=w23_scales[:, a * N + m * P : a * N + (m + 1) * P],
                rhs=words.bitcast(FP8X4),
                rhs_scale=scales,
                start=(a == 1),
                stop=(a == 0),
            )

        def z_products(v0, v1):
            words, scales = quantise(z_grouped[:, v0:v1, :].rearrange("p v t -> p (v t)"), v1 - v0, f"z{v0}")
            for piece, (a, b) in enumerate(PIECES):
                if v0 <= a < v1:
                    for m in range(2):
                        product(piece, m, 1, words[:, a - v0 : b - v0], scales[:, a - v0 : b - v0])

        def centre_products(piece, cg):
            v0, v1 = PIECES[piece]
            words, scales = quantise(cg[:].rearrange("p v t -> p (v t)"), v1 - v0, f"c{piece}")
            for m in range(2):
                product(piece, m, 0, words[:], scales[:])

        def store(piece, on_vector=()):
            v0, v1 = PIECES[piece]
            for m in range(2):
                res = keep.tile([P, v1 - v0], F32, name=f"res{piece}_{m}")
                if m in on_vector:
                    nc.vector.tensor_copy(res[:], acc[piece, m][:])
                else:
                    nc.scalar.copy(res[:], acc[piece, m][:])
                nc.sync.dma_start(out[m * P : (m + 1) * P, v0:v1], res[:])

        c_planes = [gather_centres(0, "nb2_0", PIECES[:1]), gather_centres(1, "nb2_1", PIECES[1:])]
        group_z(*HALVES[0])
        c_grouped0 = group_centres(VEC, 0)
        z_products(*HALVES[0])
        centre_products(0, c_grouped0)
        group_z(*HALVES[1])
        c_grouped2 = group_centres(SCA, 2)
        store(0)
        c_grouped1 = group_centres(VEC, 1)
        z_products(*HALVES[1])
        centre_products(1, c_grouped1)
        centre_products(2, c_grouped2)
        store(1, (1,))
        store(2, (1,))
